import numpy as np
import ml_dtypes


def mxq(x, axis, fmt="e4m3"):
    dtype, down = {"e4m3": (ml_dtypes.float8_e4m3fn, 7), "e5m2": (ml_dtypes.float8_e5m2, 14)}[fmt]
    v = np.moveaxis(np.asarray(x, np.float32).astype(ml_dtypes.bfloat16).astype(np.float64), axis, -1)
    blocks = v.reshape(v.shape[:-1] + (-1, 32))
    amax = np.abs(blocks).max(-1, keepdims=True)
    byte = np.maximum(np.where(amax > 0, np.frexp(amax)[1] - 1 + 127, 0) - down, 1)
    scale = np.exp2(byte - 127.0)
    codes = (blocks / scale).astype(np.float32).astype(dtype).astype(np.float64)
    return np.moveaxis((codes * scale).reshape(v.shape), -1, axis)


WIDE = False


def mx_kscale(k):
    if not WIDE:
        return np.ones(k)
    levels = np.array([10, -10, 5, -5, 0])
    if k % 512:
        return np.exp2(np.random.permutation(np.resize(levels, k // 32))).repeat(32)
    a = np.empty((k // 512, 16))
    for p in range(k // 512):
        a[p, :8] = np.random.permutation(np.resize(levels, 8))
        for g in range(8):
            far = levels[np.abs(levels - a[p, g]) >= 10]
            a[p, g + 8] = far[np.random.randint(len(far))]
    return np.exp2(a.ravel()).repeat(32)


BF16 = ml_dtypes.bfloat16


def bf(x):
    return np.asarray(x, np.float32).astype(BF16)


def f64(x):
    return np.asarray(x).astype(np.float64)

def planes(Y):
    n, m = Y.shape
    b = f64(bf(Y)).reshape(n // 32, 32, m)
    amax = np.abs(b).max(1)
    byte = np.clip(np.where(amax > 0, np.frexp(amax)[1] - 1 + 127 - 7, 1), 1, 254)
    codes = (b * np.exp2(127.0 - byte)[:, None, :]).reshape(n, m).astype(np.float32).astype(ml_dtypes.float8_e4m3fn).view(np.uint8)
    words = codes.reshape(n // 512, 128, 4, m).transpose(0, 1, 3, 2)
    return np.ascontiguousarray(words), np.ascontiguousarray(byte.astype(np.uint8).reshape(n // 512, 16, m))


S, K, R, C, D = 1024, 2048, 1024, 2, 3
KAPPA = 6.0
HEIGHT = 5.0
HALF = 1.5

def setup_inputs():
    s = mx_kscale(K)
    points = np.random.uniform(-HALF, HALF, (K, 1, D))
    receivers = np.random.uniform(-HALF, HALF, (1, R, D))
    receivers[:, :, -1] += HEIGHT
    dist = np.sqrt(np.square(points - receivers).sum(axis=-1))
    green = np.stack([np.cos(KAPPA * dist), np.sin(KAPPA * dist)], axis=-1) / (4.0 * np.pi * dist[:, :, None])
    strength = 2.0 * np.exp(0.8 * np.random.randn(S, 1))
    pressure = strength * np.random.randn(S, K)
    return {
        "pressure": bf(pressure * s),
        "green": bf(green / s[:, None, None]),
        "absorption": bf(np.random.uniform(0.05, 0.3, S)),
        "path": bf(np.sqrt(np.square(receivers[0]).sum(axis=-1))),
        "log_gain": bf(0.4 * np.random.randn(R)),
    }

def reference(pressure, green, absorption, path, log_gain):
    p = mxq(f64(pressure), 1, "e4m3")
    g = mxq(f64(green).reshape(K, R * C), 0, "e4m3")
    u = (p @ g).reshape(S, R, C)
    y = u * np.exp(f64(log_gain)[None, :, None] - f64(absorption)[:, None, None] * f64(path)[None, :, None])
    Y = y.reshape(S, R * C)
    words, scales = planes(Y)
    return y, words, scales

@@ -1,0 +1,333 @@
+from contextlib import ExitStack
+
+import concourse.mybir as mybir
+from concourse.masks import make_identity
+
+S, K, R = 1024, 2048, 1024
+N = 2 * R
+FLOPS = 2 * S * K * N
+
+F32 = mybir.dt.float32
+BF16 = mybir.dt.bfloat16
+I32 = mybir.dt.int32
+U32 = mybir.dt.uint32
+U8 = mybir.dt.uint8
+FP8X4 = mybir.dt.float8_e4m3fn_x4
+ALU = mybir.AluOpType
+ACT = mybir.ActivationFunctionType
+
+P = 128
+PACK = 4
+K_PASS = P * PACK
+PASSES = K // K_PASS
+GROUPS = S // K_PASS
+STRIP = 512
+STRIPS = N // STRIP
+BANK = 512
+RUN = 4
+VECTOR_COLS_HEAD = 256
+VECTOR_COLS_MID = 224
+VECTOR_COLS = 208
+POOL_COLS = 0
+TAIL_COLS = 168
+FACTOR_BUFS = 4
+WOVEN_BUFS = 6
+HEAD_ARG = 3.05
+TURN_LEAD = 1.5
+DRAIN_B = 0.2
+DVE_DRAIN = 4
+QP = 1.6
+QG = 1.3
+WINDOW0 = 9.2
+
+
+def tile_green_shot_response_g2_kernel(tc, pressure, green, absorption, path, log_gain, out_0, out_1, out_2):
+    nc = tc.nc
+    green_kn = green.rearrange("k r c -> k (r c)")
+    y_hbm = out_0.rearrange("(g p t) r c -> g p t (r c)", p=P, t=PACK)
+    words_hbm = out_1.rearrange("g p m t -> g p (m t)").bitcast(I32)
+    scales_hbm = out_2.bitcast(I32)
+    shots_hbm = pressure.rearrange("(g p t) k -> g t p k", p=P, t=PACK)
+
+    with ExitStack() as ctx:
+        keep = ctx.enter_context(tc.tile_pool(name="keep", bufs=1))
+        psum = ctx.enter_context(tc.psum_pool(name="psum", bufs=1))
+        ctx.enter_context(tc.manual_schedule(engines={mybir.EngineType.SP}))
+
+        def bank_tile(index):
+            return psum.tile([P, BANK], F32, name="bank%d" % index)
+
+        def interleave(copy, woven, rows, first, last):
+            copy(
+                out=woven[:, first * PACK : last * PACK].rearrange("p (c i t) -> p c t i", i=RUN, t=PACK),
+                in_=rows[:, :, first:last].rearrange("p t (c i) -> p c t i", i=RUN),
+            )
+
+        def pool_copy(out, in_):
+            nc.gpsimd.tensor_scalar(out=out, in0=in_, scalar1=1.0, scalar2=0.0, op0=ALU.mult, op1=ALU.add)
+
+        identity = keep.tile([P, P], F32, name="identity")
+        make_identity(nc, identity[:])
+
+        path_rows = keep.tile([P, STRIPS, 2], BF16, name="path_rows")
+        nc.scalar.dma_start(out=path_rows[:], in_=path.rearrange("(n p e) -> p n e", p=P, e=2))
+        gain_rows = keep.tile([P, STRIPS, 2], BF16, name="gain_rows")
+        nc.scalar.dma_start(out=gain_rows[:], in_=log_gain.rearrange("(n p e) -> p n e", p=P, e=2))
+        absorb = keep.tile([P, GROUPS, PACK], BF16, name="absorb")
+        nc.scalar.dma_start(out=absorb[:], in_=absorption.rearrange("(g p t) -> p g t", p=P, t=PACK))
+
+        raw = {}
+
+        def load(item):
+            kind, a, b = item
+            if kind == "shots":
+                tile = keep.tile([P, K], BF16, name="shots_raw", bufs=8)
+                nc.sync.dma_start(out=tile[:], in_=shots_hbm[a, b])
+            else:
+                tile = keep.tile([P, PACK, STRIP], BF16, name="green_raw", bufs=10)
+                rows = green_kn[b * K_PASS : (b + 1) * K_PASS, a * STRIP : (a + 1) * STRIP]
+                nc.sync.dma_start(out=tile[:], in_=rows.rearrange("(p j) w -> p j w", j=PACK))
+            raw[item] = tile
+
+        head_items = []
+        for pair in range(2):
+            head_items.extend([("shots", 0, pair), ("green", 0, 2 * pair), ("green", 0, 2 * pair + 1)])
+        head_items.extend([("shots", 0, 2), ("shots", 0, 3)])
+        for t in range(PACK):
+            head_items.extend([("shots", 1, t), ("green", 1, t)])
+        for item in head_items:
+            load(item)
+
+        spreads = {}
+
+        def spread(strips, bank_index, copy):
+            bank = bank_tile(bank_index)
+            tile = keep.tile([P, len(strips), 2, STRIP // 2], BF16, name="spread%d" % strips[0])
+            for place, n in enumerate(strips):
+                for which, rows in enumerate((path_rows, gain_rows)):
+                    words = rows[:].rearrange("p n e -> p (n e)").bitcast(F32)
+                    first = (2 * place + which) * P
+                    nc.tensor.transpose(bank[:, first : first + P], words[:, n : n + 1].to_broadcast([P, P]), identity[:])
+                spreads[n] = tile[:, place]
+            copy(out=tile[:].rearrange("p n w r -> p (n w r)").bitcast(F32), in_=bank[:, : 2 * P * len(strips)])
+
+        y_scales = keep.tile([P, GROUPS, N], U8, name="y_scales", align_bytes=64)
+
+        units = [(g, n * STRIP, STRIP) for n in range(STRIPS) for g in range(GROUPS)]
+        last_g, last_col, last_width = units.pop()
+        units.extend([(last_g, last_col, last_width // 2), (last_g, last_col + last_width // 2, last_width // 2)])
+        jobs = []
+        for unit in units:
+            per_bank = BANK // unit[2]
+            for t0 in range(0, PACK, per_bank):
+                jobs.append((unit, tuple(range(t0, t0 + per_bank))))
+
+        woven = {}
+        codes = {}
+        factors = {}
+        y_tiles = {}
+        y_woven = {}
+        job_banks = {}
+        passes_done = {}
+        turned = {}
+
+        def woven_tile(item):
+            if item not in woven:
+                woven[item] = keep.tile([P, K], BF16, name="woven", bufs=WOVEN_BUFS, align_bytes=64)
+            return woven[item]
+
+        def turn(item, half):
+            words = raw[item][:].bitcast(F32)
+            bank = bank_tile(4 + (2 * item[2] + half) % 4)
+            for j in range(4):
+                first = 256 * (2 * half + j // 2) + j % 2
+                nc.tensor.transpose(bank[:, j * P : (j + 1) * P], words[:, first : first + 255 : 2], identity[:])
+            turned[(item, half)] = bank
+
+        def drain(item, half, copy):
+            copy(
+                out=woven_tile(item)[:, half * 1024 : (half + 1) * 1024].bitcast(F32).rearrange("p (c m u) -> p c m u", c=2, u=2),
+                in_=turned[(item, half)][:].rearrange("p (c u m) -> p c m u", c=2, u=2),
+            )
+
+        def weave(item, copy, first, last):
+            interleave(copy, woven_tile(item), raw[item], first, last)
+
+        def quantize(item):
+            count = 8 if item[0] == "shots" else 16
+            words = keep.tile([P, STRIP], U32, name=item[0] + "_codes", bufs=count, align_bytes=64)
+            scales = keep.tile([P, STRIP], U8, name=item[0] + "_scales", bufs=count, align_bytes=64)
+            nc.vector.quantize_mx(out=words[:].bitcast(FP8X4), scales=scales[:], in_=woven[item][:])
+            codes[item] = (words, scales)
+
+        def multiply(job, c):
+            (g, col, width), slots = job
+            if job not in job_banks:
+                index = jobs.index(job)
+                job_banks[job] = bank_tile(index % 4 if index < 8 else (index + 4) % 8)
+            n, first = divmod(col, STRIP)
+            return_cols = slice(first, first + width)
+            g_words, g_scales = codes[("green", n, c[1])]
+            s_words, s_scales = codes[("shots", g, slots[c[0]])]
+            shots = slice(c[1] * P, (c[1] + 1) * P)
+            done = passes_done.setdefault((job, c[0]), [])
+            nc.tensor.matmul_mx(
+                out=job_banks[job][:, c[0] * width : (c[0] + 1) * width],
+                lhsT=s_words[:, shots].bitcast(FP8X4),
+                lhsT_scale=s_scales[:, shots],
+                rhs=g_words[:, return_cols].bitcast(FP8X4),
+                rhs_scale=g_scales[:, return_cols],
+                start=len(done) == 0,
+                stop=len(done) == PASSES - 1,
+            )
+            done.append(c[1])
+
+        def exponent(job):
+            unit, slots = job
+            g, col, width = unit
+            if unit not in factors:
+                factors[unit] = keep.tile([P, PACK, width // 2], F32, name="factor", bufs=FACTOR_BUFS)
+            receivers = slice(col % STRIP // 2, (col % STRIP + width) // 2)
+            for t in slots:
+                nc.vector.scalar_tensor_tensor(
+                    out=factors[unit][:, t, :],
+                    in0=spreads[col // STRIP][:, 0, receivers],
+                    scalar=absorb[:, g, t : t + 1],
+                    in1=spreads[col // STRIP][:, 1, receivers],
+                    op0=ALU.mult,
+                    op1=ALU.subtract,
+                )
+
+        def exponential(unit, t):
+            pair = factors[unit][:, t : t + 2, :]
+            nc.scalar.activation(out=pair, in_=pair, func=ACT.Exp, scale=-1.0)
+
+        def scale_out(job):
+            unit, slots = job
+            g, col, width = unit
+            if unit not in y_tiles:
+                y_tiles[unit] = keep.tile([P, PACK, width], F32, name="y", bufs=3)
+            ts = slice(slots[0], slots[-1] + 1)
+            nc.vector.tensor_tensor(
+                out=y_tiles[unit][:, ts, :].rearrange("p t (r c) -> p t r c", c=2),
+                in0=job_banks[job][:].rearrange("p (t r c) -> p t r c", t=len(slots), c=2),
+                in1=factors[unit][:, ts, :].unsqueeze(3).to_broadcast([P, len(slots), width // 2, 2]),
+                op=ALU.mult,
+            )
+            if slots[-1] == PACK - 1:
+                nc.sync.dma_start(out=y_hbm[g, :, :, col : col + width], in_=y_tiles[unit][:])
+
+        def weave_result(unit, copy, first, last):
+            if unit not in y_woven:
+                y_woven[unit] = keep.tile([P, PACK * unit[2]], BF16, name="y_woven", bufs=1 if unit[2] == STRIP else 2, tag="y_woven%d" % unit[2], align_bytes=64)
+            interleave(copy, y_woven[unit], y_tiles[unit], first, last)
+
+        def quantize_result(unit):
+            g, col, width = unit
+            words = keep.tile([P, width], U32, name="y_codes", bufs=3, align_bytes=64)
+            nc.vector.quantize_mx(out=words[:].bitcast(FP8X4), scales=y_scales[:, g, col : col + width], in_=y_woven[unit][:])
+            nc.sync.dma_start(out=words_hbm[g, :, col : col + width], in_=words[:].bitcast(I32))
+
+        def store_scales(first, last, queues):
+            for q in range(4):
+                queues[q % len(queues)].dma_start(
+                    out=scales_hbm[:, 4 * q : 4 * q + 4, first // 4 : last // 4].rearrange("g r m -> r g m"),
+                    in_=y_scales[32 * q : 32 * q + 4, :, first:last].bitcast(I32),
+                )
+
+        plan = []
+
+        def at(slot, step, *args):
+            plan.append((slot, len(plan), step, args))
+
+        def multiply_all(job):
+            for place in range(len(job[1])):
+                for c in range(PASSES):
+                    multiply(job, (place, c))
+
+        def plan_factors(unit, slot, exp_slot):
+            for job in jobs:
+                if job[0] == unit:
+                    at(slot, exponent, job)
+            for t in (0, 2):
+                at(exp_slot, exponential, unit, t)
+
+        at(-2, spread, [0], 0, nc.vector.tensor_copy)
+        at(-1.4, spread, [1, 2], 1, nc.vector.tensor_copy)
+        at(-1.4, spread, [3], 2, nc.vector.tensor_copy)
+        at(-1.9, exponent, jobs[0])
+        at(-1.9, exponent, jobs[1])
+        at(-1.9, exponential, units[0], 0)
+        at(HEAD_ARG, exponent, jobs[2])
+        at(HEAD_ARG, exponent, jobs[3])
+        at(HEAD_ARG + 0.5, exponential, units[0], 2)
+        quantized_at = {}
+        for slot, item in enumerate(head_items):
+            kind, g, t = item
+            if kind == "shots":
+                at(slot - TURN_LEAD, turn, item, 0)
+                at(slot - TURN_LEAD, turn, item, 1)
+                at(slot + 0.1, drain, item, 0, nc.scalar.copy)
+                at(slot + DRAIN_B, drain, item, 1, nc.vector.tensor_copy if (g == 0 and t >= DVE_DRAIN) else nc.scalar.copy)
+                quantized_at[item] = slot + QP
+            else:
+                vector_cols = VECTOR_COLS_HEAD if g == 0 else VECTOR_COLS_MID
+                at(slot, weave, item, nc.scalar.copy, vector_cols, STRIP)
+                at(slot, weave, item, nc.vector.tensor_copy, 0, vector_cols)
+                quantized_at[item] = slot + QG
+            at(quantized_at[item], quantize, item)
+        for j, job in enumerate(jobs[: 2 * PACK]):
+            g, t = divmod(j, PACK)
+            for c in range(PASSES):
+                at(max(quantized_at[("shots", g, t)], quantized_at[("green", 0, c)]) + 0.01, multiply, job, (0, c))
+            if g == 0:
+                at(WINDOW0, scale_out, job)
+            else:
+                at(2 * j + 2.35, exponent, job)
+                if t % 2:
+                    at(2 * j + 2.9, exponential, units[1], t - 1)
+        for c in range(PASSES):
+            at(4, load, ("green", STRIPS - 2, c))
+            at(13, load, ("green", STRIPS - 1, c))
+
+        whole = [unit for unit in units if unit[2] == STRIP]
+        for u in range(1, len(whole) + 1):
+            slot = 20 + u
+            these = jobs[PACK * u : PACK * (u + 1)]
+            for job in jobs[PACK * (u + 1) : PACK * (u + 2)]:
+                at(slot, multiply_all, job)
+            before = units[u - 1]
+            if POOL_COLS:
+                at(slot + 0.1, weave_result, before, pool_copy, 0, POOL_COLS)
+            if POOL_COLS < STRIP:
+                at(slot + 0.1, weave_result, before, nc.scalar.copy, POOL_COLS, STRIP)
+            if u < len(whole):
+                for job in these:
+                    at(slot + 0.05, scale_out, job)
+                for unit in units[u + 1 : u + 2 if u + 1 < len(whole) else u + 3]:
+                    plan_factors(unit, slot + 0.2, slot + 0.8)
+                at(slot + 0.9, quantize_result, before)
+            strip, step = divmod(u - 1, 2)
+            if strip + 2 < STRIPS:
+                for number in range(2):
+                    item = ("green", strip + 2, 2 * step + number)
+                    at(slot + 0.3 + 0.1 * number, weave, item, nc.scalar.copy, VECTOR_COLS, STRIP)
+                    at(slot + 0.3 + 0.1 * number, weave, item, nc.vector.tensor_copy, 0, VECTOR_COLS)
+                    at(slot + 0.5 + 0.1 * number, quantize, item)
+        slot = 20 + len(whole)
+        first_half, second_half = units[-2:]
+        at(slot + 0.2, scale_out, jobs[-4])
+        at(slot + 0.2, scale_out, jobs[-3])
+        at(slot + 0.3, store_scales, 0, N - STRIP, [nc.sync])
+        at(slot + 0.3, weave_result, first_half, nc.scalar.copy, 0, 256)
+        at(slot + 0.4, scale_out, jobs[-2])
+        at(slot + 0.45, quantize_result, whole[-1])
+        at(slot + 0.5, scale_out, jobs[-1])
+        at(slot + 0.6, quantize_result, first_half)
+        at(slot + 0.7, weave_result, second_half, nc.scalar.copy, TAIL_COLS, 256)
+        at(slot + 0.7, weave_result, second_half, nc.vector.tensor_copy, 0, TAIL_COLS)
+        at(slot + 0.8, quantize_result, second_half)
+        at(slot + 0.9, store_scales, N - STRIP, N, [nc.scalar, nc.sync])
+
+        for slot, number, step, args in sorted(plan, key=lambda entry: entry[:2]):
+            step(*args)

@@ -25,20 +25,32 @@ STRIP = 512
 STRIPS = N // STRIP
 BANK = 512
 RUN = 4
-VECTOR_COLS_HEAD = 256
-VECTOR_COLS_MID = 224
-VECTOR_COLS = 208
-POOL_COLS = 0
-TAIL_COLS = 168
-FACTOR_BUFS = 4
-WOVEN_BUFS = 6
-HEAD_ARG = 3.05
-TURN_LEAD = 1.5
-DRAIN_B = 0.2
-DVE_DRAIN = 4
-QP = 1.6
-QG = 1.3
-WINDOW0 = 9.2
+VECTOR_COLS_HEAD = 352
+VECTOR_COLS_MID = 256
+VECTOR_COLS = 0
+POOL_COLS = 400
+TAIL_COLS = 160
+EARLY_GREEN = 10
+EARLY_UNITS = 3
+PER_ROUND = (2, 2, 2, 0, 0, 0, 0)
+Y_ROUND = (0, 0, 0, 2, 2, 2, 1)
+Y_COLS = 64
+Y_LAG = 1.04
+EXP_AT = 0.5
+Y_BUFS = 5
+SCALES_AT = 0.92
+STORE_SLOTS = 2
+POOL_LAST = 224
+ARG_AT = 0.07
+QP = 0.52
+QG = 1.1
+WINDOW0 = 2.3
+ARGS_PER_BEAT = 2
+ARG_SKIP = 1
+EXP_LAG = 0.5
+SPREAD_AT = 0.505
+TURN_LEAD = 0.49
+WOVEN_BUFS = 5
 
 
 def tile_green_shot_response_g2_kernel(tc, pressure, green, absorption, path, log_gain, out_0, out_1, out_2):
@@ -50,9 +62,9 @@ def tile_green_shot_response_g2_kernel(tc, pressure, green, absorption, path, lo
     shots_hbm = pressure.rearrange("(g p t) k -> g t p k", p=P, t=PACK)
 
     with ExitStack() as ctx:
-        keep = ctx.enter_context(tc.tile_pool(name="keep", bufs=1))
+        sbuf = ctx.enter_context(tc.tile_pool(name="sbuf", bufs=1))
         psum = ctx.enter_context(tc.psum_pool(name="psum", bufs=1))
-        ctx.enter_context(tc.manual_schedule(engines={mybir.EngineType.SP}))
+        ctx.enter_context(tc.manual_schedule())
 
         def bank_tile(index):
             return psum.tile([P, BANK], F32, name="bank%d" % index)
@@ -63,58 +75,38 @@ def tile_green_shot_response_g2_kernel(tc, pressure, green, absorption, path, lo
                 in_=rows[:, :, first:last].rearrange("p t (c i) -> p c t i", i=RUN),
             )
 
-        def pool_copy(out, in_):
-            nc.gpsimd.tensor_scalar(out=out, in0=in_, scalar1=1.0, scalar2=0.0, op0=ALU.mult, op1=ALU.add)
+        def pool_interleave(woven, rows, last):
+            nc.gpsimd.tensor_scalar(
+                out=woven[:, : last * PACK].rearrange("p (c t) -> p c t", t=PACK),
+                in0=rows[:, :, :last].rearrange("p t c -> p c t"),
+                scalar1=1.0,
+                scalar2=0.0,
+                op0=ALU.mult,
+                op1=ALU.add,
+            )
 
-        identity = keep.tile([P, P], F32, name="identity")
+        identity = sbuf.tile([P, P], F32, name="identity")
         make_identity(nc, identity[:])
 
-        path_rows = keep.tile([P, STRIPS, 2], BF16, name="path_rows")
-        nc.scalar.dma_start(out=path_rows[:], in_=path.rearrange("(n p e) -> p n e", p=P, e=2))
-        gain_rows = keep.tile([P, STRIPS, 2], BF16, name="gain_rows")
-        nc.scalar.dma_start(out=gain_rows[:], in_=log_gain.rearrange("(n p e) -> p n e", p=P, e=2))
-        absorb = keep.tile([P, GROUPS, PACK], BF16, name="absorb")
+        gain_rows = sbuf.tile([P, R // P], BF16, name="gain_rows")
+        nc.scalar.dma_start(out=gain_rows[:], in_=log_gain.rearrange("(p m) -> p m", p=P))
+        path_rows = sbuf.tile([P, R // P], BF16, name="path_rows")
+        nc.scalar.dma_start(out=path_rows[:], in_=path.rearrange("(p m) -> p m", p=P))
+        absorb = sbuf.tile([P, GROUPS, PACK], BF16, name="absorb")
         nc.scalar.dma_start(out=absorb[:], in_=absorption.rearrange("(g p t) -> p g t", p=P, t=PACK))
+        early_scales = sbuf.tile([P, GROUPS, N // 2], U8, name="early_scales", align_bytes=64)
+        late_scales = sbuf.tile([P, GROUPS, N // 2], U8, name="late_scales", align_bytes=64)
+        y_scales = (early_scales, late_scales)
 
-        raw = {}
-
-        def load(item):
-            kind, a, b = item
-            if kind == "shots":
-                tile = keep.tile([P, K], BF16, name="shots_raw", bufs=8)
-                nc.sync.dma_start(out=tile[:], in_=shots_hbm[a, b])
-            else:
-                tile = keep.tile([P, PACK, STRIP], BF16, name="green_raw", bufs=10)
-                rows = green_kn[b * K_PASS : (b + 1) * K_PASS, a * STRIP : (a + 1) * STRIP]
-                nc.sync.dma_start(out=tile[:], in_=rows.rearrange("(p j) w -> p j w", j=PACK))
-            raw[item] = tile
-
-        head_items = []
-        for pair in range(2):
-            head_items.extend([("shots", 0, pair), ("green", 0, 2 * pair), ("green", 0, 2 * pair + 1)])
-        head_items.extend([("shots", 0, 2), ("shots", 0, 3)])
-        for t in range(PACK):
-            head_items.extend([("shots", 1, t), ("green", 1, t)])
-        for item in head_items:
-            load(item)
-
-        spreads = {}
-
-        def spread(strips, bank_index, copy):
-            bank = bank_tile(bank_index)
-            tile = keep.tile([P, len(strips), 2, STRIP // 2], BF16, name="spread%d" % strips[0])
-            for place, n in enumerate(strips):
-                for which, rows in enumerate((path_rows, gain_rows)):
-                    words = rows[:].rearrange("p n e -> p (n e)").bitcast(F32)
-                    first = (2 * place + which) * P
-                    nc.tensor.transpose(bank[:, first : first + P], words[:, n : n + 1].to_broadcast([P, P]), identity[:])
-                spreads[n] = tile[:, place]
-            copy(out=tile[:].rearrange("p n w r -> p (n w r)").bitcast(F32), in_=bank[:, : 2 * P * len(strips)])
-
-        y_scales = keep.tile([P, GROUPS, N], U8, name="y_scales", align_bytes=64)
+        shot_items = [("shots", g, t) for g in range(GROUPS) for t in range(PACK)]
+        green_items = [("green", n, c) for n in range(STRIPS) for c in range(PASSES)]
+        beat_green = [green_items[:2], green_items[2:4]] + [[item] for item in green_items[4:EARLY_GREEN]]
+        late_items = green_items[EARLY_GREEN:]
+        gate_item = green_items[EARLY_GREEN - 1]
 
         units = [(g, n * STRIP, STRIP) for n in range(STRIPS) for g in range(GROUPS)]
         last_g, last_col, last_width = units.pop()
+        whole = list(units)
         units.extend([(last_g, last_col, last_width // 2), (last_g, last_col + last_width // 2, last_width // 2)])
         jobs = []
         for unit in units:
@@ -122,30 +114,61 @@ def tile_green_shot_response_g2_kernel(tc, pressure, green, absorption, path, lo
             for t0 in range(0, PACK, per_bank):
                 jobs.append((unit, tuple(range(t0, t0 + per_bank))))
 
+        gated = [gate_item]
+        raw = {}
         woven = {}
+        turned = {}
         codes = {}
         factors = {}
         y_tiles = {}
         y_woven = {}
         job_banks = {}
         passes_done = {}
-        turned = {}
+
+        def load(item):
+            kind, a, b = item
+            if kind == "shots":
+                tile = sbuf.tile([P, K], BF16, name="shots_raw", bufs=6)
+                nc.sync.dma_start(out=tile[:], in_=shots_hbm[a, b])
+            else:
+                tile = sbuf.tile([P, PACK, STRIP], BF16, name="green_raw", bufs=8)
+                rows = green_kn[b * K_PASS : (b + 1) * K_PASS, a * STRIP : (a + 1) * STRIP]
+                nc.sync.dma_start(out=tile[:], in_=rows.rearrange("(p j) w -> p j w", j=PACK))
+            raw[item] = tile
+
+        path_bank = bank_tile(7)
+        gain_all = sbuf.tile([P, R], BF16, name="gain_all")
+
+        gain_bank = bank_tile(1)
+
+        def spread(rows, bank):
+            words = rows[:].bitcast(F32)
+            count = R // P // 2
+            for m in range(count):
+                nc.tensor.transpose(bank[:, m::count], words[:, m : m + 1].to_broadcast([P, P]), identity[:])
+
+        def fetch_gain(first, last):
+            nc.vector.tensor_copy(out=gain_all[:].bitcast(F32)[:, first:last], in_=gain_bank[:, first:last])
 
         def woven_tile(item):
             if item not in woven:
-                woven[item] = keep.tile([P, K], BF16, name="woven", bufs=WOVEN_BUFS, align_bytes=64)
+                if item in gated:
+                    woven[item] = sbuf.tile([P, K], BF16, name="gated", bufs=1, align_bytes=64)
+                else:
+                    woven[item] = sbuf.tile([P, K], BF16, name="woven", bufs=WOVEN_BUFS, align_bytes=64)
             return woven[item]
 
-        def turn(item, half):
+        def turn(item):
             words = raw[item][:].bitcast(F32)
-            bank = bank_tile(4 + (2 * item[2] + half) % 4)
-            for j in range(4):
-                first = 256 * (2 * half + j // 2) + j % 2
-                nc.tensor.transpose(bank[:, j * P : (j + 1) * P], words[:, first : first + 255 : 2], identity[:])
-            turned[(item, half)] = bank
+            for half in range(2):
+                bank = bank_tile(4 + len(turned) % 3)
+                for j in range(4):
+                    first = 256 * (2 * half + j // 2) + j % 2
+                    nc.tensor.transpose(bank[:, j * P : (j + 1) * P], words[:, first : first + 255 : 2], identity[:])
+                turned[(item, half)] = bank
 
-        def drain(item, half, copy):
-            copy(
+        def drain(item, half):
+            nc.scalar.copy(
                 out=woven_tile(item)[:, half * 1024 : (half + 1) * 1024].bitcast(F32).rearrange("p (c m u) -> p c m u", c=2, u=2),
                 in_=turned[(item, half)][:].rearrange("p (c u m) -> p c m u", c=2, u=2),
             )
@@ -153,60 +176,68 @@ def tile_green_shot_response_g2_kernel(tc, pressure, green, absorption, path, lo
         def weave(item, copy, first, last):
             interleave(copy, woven_tile(item), raw[item], first, last)
 
+        def pool_weave(item, last):
+            pool_interleave(woven_tile(item), raw[item], last)
+
         def quantize(item):
-            count = 8 if item[0] == "shots" else 16
-            words = keep.tile([P, STRIP], U32, name=item[0] + "_codes", bufs=count, align_bytes=64)
-            scales = keep.tile([P, STRIP], U8, name=item[0] + "_scales", bufs=count, align_bytes=64)
+            count = len(shot_items) if item[0] == "shots" else len(green_items)
+            words = sbuf.tile([P, STRIP], U32, name=item[0] + "_codes", bufs=count, align_bytes=64)
+            scales = sbuf.tile([P, STRIP], U8, name=item[0] + "_scales", bufs=count, align_bytes=64)
             nc.vector.quantize_mx(out=words[:].bitcast(FP8X4), scales=scales[:], in_=woven[item][:])
             codes[item] = (words, scales)
 
-        def multiply(job, c):
+        def multiply(job, place, c):
             (g, col, width), slots = job
             if job not in job_banks:
                 index = jobs.index(job)
-                job_banks[job] = bank_tile(index % 4 if index < 8 else (index + 4) % 8)
+                job_banks[job] = bank_tile(index % 4 if index < 8 else (index - 4) % 7)
             n, first = divmod(col, STRIP)
-            return_cols = slice(first, first + width)
-            g_words, g_scales = codes[("green", n, c[1])]
-            s_words, s_scales = codes[("shots", g, slots[c[0]])]
-            shots = slice(c[1] * P, (c[1] + 1) * P)
-            done = passes_done.setdefault((job, c[0]), [])
+            cols = slice(first, first + width)
+            green_words, green_scales = codes[("green", n, c)]
+            shot_words, shot_scales = codes[("shots", g, slots[place])]
+            shots = slice(c * P, (c + 1) * P)
+            done = passes_done.setdefault((job, place), [])
             nc.tensor.matmul_mx(
-                out=job_banks[job][:, c[0] * width : (c[0] + 1) * width],
-                lhsT=s_words[:, shots].bitcast(FP8X4),
-                lhsT_scale=s_scales[:, shots],
-                rhs=g_words[:, return_cols].bitcast(FP8X4),
-                rhs_scale=g_scales[:, return_cols],
+                out=job_banks[job][:, place * width : (place + 1) * width],
+                lhsT=shot_words[:, shots].bitcast(FP8X4),
+                lhsT_scale=shot_scales[:, shots],
+                rhs=green_words[:, cols].bitcast(FP8X4),
+                rhs_scale=green_scales[:, cols],
                 start=len(done) == 0,
                 stop=len(done) == PASSES - 1,
             )
-            done.append(c[1])
+            done.append(c)
+
+        def multiply_all(job):
+            for place in range(len(job[1])):
+                for c in range(PASSES):
+                    multiply(job, place, c)
 
         def exponent(job):
             unit, slots = job
             g, col, width = unit
             if unit not in factors:
-                factors[unit] = keep.tile([P, PACK, width // 2], F32, name="factor", bufs=FACTOR_BUFS)
-            receivers = slice(col % STRIP // 2, (col % STRIP + width) // 2)
+                factors[unit] = sbuf.tile([P, PACK, width // 2], F32, name="factor", bufs=EARLY_UNITS + 1)
+            receivers = slice(col // 2, (col + width) // 2)
             for t in slots:
                 nc.vector.scalar_tensor_tensor(
                     out=factors[unit][:, t, :],
-                    in0=spreads[col // STRIP][:, 0, receivers],
+                    in0=path_bank[:].bitcast(BF16)[:, receivers],
                     scalar=absorb[:, g, t : t + 1],
-                    in1=spreads[col // STRIP][:, 1, receivers],
+                    in1=gain_all[:, receivers],
                     op0=ALU.mult,
                     op1=ALU.subtract,
                 )
 
-        def exponential(unit, t):
-            pair = factors[unit][:, t : t + 2, :]
-            nc.scalar.activation(out=pair, in_=pair, func=ACT.Exp, scale=-1.0)
+        def exponential(unit, first, last):
+            part = factors[unit][:, first:last, :]
+            nc.scalar.activation(out=part, in_=part, func=ACT.Exp, scale=-1.0)
 
         def scale_out(job):
             unit, slots = job
             g, col, width = unit
             if unit not in y_tiles:
-                y_tiles[unit] = keep.tile([P, PACK, width], F32, name="y", bufs=3)
+                y_tiles[unit] = sbuf.tile([P, PACK, width], F32, name="y", bufs=Y_BUFS)
             ts = slice(slots[0], slots[-1] + 1)
             nc.vector.tensor_tensor(
                 out=y_tiles[unit][:, ts, :].rearrange("p t (r c) -> p t r c", c=2),
@@ -214,25 +245,39 @@ def tile_green_shot_response_g2_kernel(tc, pressure, green, absorption, path, lo
                 in1=factors[unit][:, ts, :].unsqueeze(3).to_broadcast([P, len(slots), width // 2, 2]),
                 op=ALU.mult,
             )
-            if slots[-1] == PACK - 1:
-                nc.sync.dma_start(out=y_hbm[g, :, :, col : col + width], in_=y_tiles[unit][:])
+            if slots[-1] % STORE_SLOTS == STORE_SLOTS - 1:
+                pair = slice(slots[-1] + 1 - STORE_SLOTS, slots[-1] + 1)
+                nc.sync.dma_start(out=y_hbm[g, :, pair, col : col + width], in_=y_tiles[unit][:, pair, :])
+
+        def result_tile(unit):
+            if unit not in y_woven:
+                if unit in gated:
+                    y_woven[unit] = sbuf.tile([P, PACK * unit[2]], BF16, name="gated", bufs=1, align_bytes=64)
+                elif unit in whole:
+                    y_woven[unit] = sbuf.tile([P, PACK * unit[2]], BF16, name="y_woven", bufs=2, align_bytes=64)
+                else:
+                    y_woven[unit] = sbuf.tile([P, PACK * unit[2]], BF16, name="last_woven", bufs=2, align_bytes=64)
+            return y_woven[unit]
 
         def weave_result(unit, copy, first, last):
-            if unit not in y_woven:
-                y_woven[unit] = keep.tile([P, PACK * unit[2]], BF16, name="y_woven", bufs=1 if unit[2] == STRIP else 2, tag="y_woven%d" % unit[2], align_bytes=64)
-            interleave(copy, y_woven[unit], y_tiles[unit], first, last)
+            interleave(copy, result_tile(unit), y_tiles[unit], first, last)
+
+        def pool_weave_result(unit, last):
+            pool_interleave(result_tile(unit), y_tiles[unit], last)
 
         def quantize_result(unit):
             g, col, width = unit
-            words = keep.tile([P, width], U32, name="y_codes", bufs=3, align_bytes=64)
-            nc.vector.quantize_mx(out=words[:].bitcast(FP8X4), scales=y_scales[:, g, col : col + width], in_=y_woven[unit][:])
+            words = sbuf.tile([P, width], U32, name="y_codes", bufs=5, align_bytes=64)
+            nc.vector.quantize_mx(out=words[:].bitcast(FP8X4), scales=y_scales[col // (N // 2)][:, g, col % (N // 2) : col % (N // 2) + width], in_=y_woven[unit][:])
             nc.sync.dma_start(out=words_hbm[g, :, col : col + width], in_=words[:].bitcast(I32))
 
-        def store_scales(first, last, queues):
+        def store_scales(half, queues):
+            first = half * N // 2
+            last = first + N // 2
             for q in range(4):
                 queues[q % len(queues)].dma_start(
                     out=scales_hbm[:, 4 * q : 4 * q + 4, first // 4 : last // 4].rearrange("g r m -> r g m"),
-                    in_=y_scales[32 * q : 32 * q + 4, :, first:last].bitcast(I32),
+                    in_=y_scales[half][32 * q : 32 * q + 4].bitcast(I32),
                 )
 
         plan = []
@@ -240,94 +285,93 @@ def tile_green_shot_response_g2_kernel(tc, pressure, green, absorption, path, lo
         def at(slot, step, *args):
             plan.append((slot, len(plan), step, args))
 
-        def multiply_all(job):
-            for place in range(len(job[1])):
-                for c in range(PASSES):
-                    multiply(job, (place, c))
-
-        def plan_factors(unit, slot, exp_slot):
-            for job in jobs:
-                if job[0] == unit:
-                    at(slot, exponent, job)
-            for t in (0, 2):
-                at(exp_slot, exponential, unit, t)
-
-        at(-2, spread, [0], 0, nc.vector.tensor_copy)
-        at(-1.4, spread, [1, 2], 1, nc.vector.tensor_copy)
-        at(-1.4, spread, [3], 2, nc.vector.tensor_copy)
-        at(-1.9, exponent, jobs[0])
-        at(-1.9, exponent, jobs[1])
-        at(-1.9, exponential, units[0], 0)
-        at(HEAD_ARG, exponent, jobs[2])
-        at(HEAD_ARG, exponent, jobs[3])
-        at(HEAD_ARG + 0.5, exponential, units[0], 2)
+        beat_green = beat_green[:-1] + [[]] * (len(shot_items) - len(beat_green)) + beat_green[-1:]
+        for k, shots in enumerate(shot_items):
+            for item in [shots] + beat_green[k]:
+                at(k - 4, load, item)
+        for number, item in enumerate(late_items):
+            at(5 + number / 2, load, item)
+        at(-3, spread, gain_rows, gain_bank)
+        at(-3, spread, path_rows, path_bank)
+        at(-3, fetch_gain, 0, P)
+        at(-2, exponent, jobs[0])
+        at(-2, exponent, jobs[1])
+        at(-2, exponential, units[0], 0, 2)
+        at(SPREAD_AT, fetch_gain, P, BANK)
+        for j, job in enumerate(jobs[2 : EARLY_UNITS * PACK]):
+            slot = 0.35 if j < 2 else (j + 0.35 if j < 6 else 6.35 + (j - 6) // ARGS_PER_BEAT)
+            at(slot, exponent, job)
+            if j % 2 and j + 2 < 2 * PACK:
+                at(slot + EXP_LAG, exponential, job[0], (j + 1) % PACK, (j + 1) % PACK + 2)
         quantized_at = {}
-        for slot, item in enumerate(head_items):
-            kind, g, t = item
-            if kind == "shots":
-                at(slot - TURN_LEAD, turn, item, 0)
-                at(slot - TURN_LEAD, turn, item, 1)
-                at(slot + 0.1, drain, item, 0, nc.scalar.copy)
-                at(slot + DRAIN_B, drain, item, 1, nc.vector.tensor_copy if (g == 0 and t >= DVE_DRAIN) else nc.scalar.copy)
-                quantized_at[item] = slot + QP
-            else:
-                vector_cols = VECTOR_COLS_HEAD if g == 0 else VECTOR_COLS_MID
-                at(slot, weave, item, nc.scalar.copy, vector_cols, STRIP)
-                at(slot, weave, item, nc.vector.tensor_copy, 0, vector_cols)
-                quantized_at[item] = slot + QG
+        for k, items in enumerate(beat_green):
+            if k < len(shot_items):
+                shots = shot_items[k]
+                at(k - TURN_LEAD, turn, shots)
+                at(k + 0.1, drain, shots, 0)
+                at(k + 0.1, drain, shots, 1)
+                quantized_at[shots] = k + QP
+            for number, item in enumerate(items):
+                share = VECTOR_COLS_HEAD if len(items) == 2 else VECTOR_COLS_MID
+                at(k + 0.2 + 0.3 * number, weave, item, nc.scalar.copy, share, STRIP)
+                at(k + 0.2 + 0.3 * number, weave, item, nc.vector.tensor_copy, 0, share)
+                quantized_at[item] = k + (0.55 + 0.3 * number if len(items) == 2 else QG)
+        quantized_at[gate_item] = len(shot_items) + 0.5
+        for item in quantized_at:
             at(quantized_at[item], quantize, item)
         for j, job in enumerate(jobs[: 2 * PACK]):
             g, t = divmod(j, PACK)
             for c in range(PASSES):
-                at(max(quantized_at[("shots", g, t)], quantized_at[("green", 0, c)]) + 0.01, multiply, job, (0, c))
+                at(max(quantized_at[("shots", g, t)], quantized_at[("green", 0, c)]) + 0.01, multiply, job, 0, c)
             if g == 0:
-                at(WINDOW0, scale_out, job)
-            else:
-                at(2 * j + 2.35, exponent, job)
-                if t % 2:
-                    at(2 * j + 2.9, exponential, units[1], t - 1)
-        for c in range(PASSES):
-            at(4, load, ("green", STRIPS - 2, c))
-            at(13, load, ("green", STRIPS - 1, c))
+                at(WINDOW0 + t, scale_out, job)
 
-        whole = [unit for unit in units if unit[2] == STRIP]
+        taken = 0
+        finished = 0
         for u in range(1, len(whole) + 1):
-            slot = 20 + u
-            these = jobs[PACK * u : PACK * (u + 1)]
+            slot = 30 + u
             for job in jobs[PACK * (u + 1) : PACK * (u + 2)]:
-                at(slot, multiply_all, job)
-            before = units[u - 1]
-            if POOL_COLS:
-                at(slot + 0.1, weave_result, before, pool_copy, 0, POOL_COLS)
-            if POOL_COLS < STRIP:
-                at(slot + 0.1, weave_result, before, nc.scalar.copy, POOL_COLS, STRIP)
+                at(slot + 0.06, multiply_all, job)
             if u < len(whole):
-                for job in these:
+                for job in jobs[PACK * u : PACK * (u + 1)]:
                     at(slot + 0.05, scale_out, job)
-                for unit in units[u + 1 : u + 2 if u + 1 < len(whole) else u + 3]:
-                    plan_factors(unit, slot + 0.2, slot + 0.8)
-                at(slot + 0.9, quantize_result, before)
-            strip, step = divmod(u - 1, 2)
-            if strip + 2 < STRIPS:
-                for number in range(2):
-                    item = ("green", strip + 2, 2 * step + number)
-                    at(slot + 0.3 + 0.1 * number, weave, item, nc.scalar.copy, VECTOR_COLS, STRIP)
-                    at(slot + 0.3 + 0.1 * number, weave, item, nc.vector.tensor_copy, 0, VECTOR_COLS)
-                    at(slot + 0.5 + 0.1 * number, quantize, item)
-        slot = 20 + len(whole)
+                for job in jobs[PACK * max(u + EARLY_UNITS - 1, EARLY_UNITS) : PACK * (u + EARLY_UNITS)]:
+                    at(slot + ARG_AT, exponent, job)
+                for unit in units[u + 1 : u + 2] if u + 1 < len(whole) else units[u + 1 :]:
+                    at(slot + EXP_AT, exponential, unit, 0, PACK)
+            work = []
+            for number in range(PER_ROUND[u - 1]):
+                work.append((late_items[taken], weave, pool_weave, quantize))
+                taken = taken + 1
+            for number in range(Y_ROUND[u - 1]):
+                work.append((units[finished], weave_result, pool_weave_result, quantize_result))
+                finished = finished + 1
+            for number, (what, by_copy, by_pool, finish) in enumerate(work):
+                if number == (min(PER_ROUND[u - 1], 2) - 1 if PER_ROUND[u - 1] else len(work) - 1):
+                    gated.append(what)
+                    pool_cols = POOL_COLS if u + 1 < len(whole) else POOL_LAST
+                    at(slot + 0.1, by_pool, what, pool_cols)
+                    if pool_cols < STRIP:
+                        at(slot + 0.1, by_copy, what, nc.scalar.copy, pool_cols, STRIP)
+                    at(slot + (0.9 if u < len(whole) else 0.55), finish, what)
+                else:
+                    at(slot + 0.11 + 0.1 * number, by_copy, what, nc.scalar.copy, VECTOR_COLS, STRIP)
+                    if VECTOR_COLS:
+                        at(slot + 0.3, by_copy, what, nc.vector.tensor_copy, 0, VECTOR_COLS)
+                    at(slot + 0.6 + 0.1 * number, finish, what)
+        slot = 30 + len(whole)
         first_half, second_half = units[-2:]
-        at(slot + 0.2, scale_out, jobs[-4])
-        at(slot + 0.2, scale_out, jobs[-3])
-        at(slot + 0.3, store_scales, 0, N - STRIP, [nc.sync])
+        at(slot - SCALES_AT, store_scales, 0, [nc.sync])
+        at(slot + 0.05, scale_out, jobs[-4])
+        at(slot + 0.05, scale_out, jobs[-3])
         at(slot + 0.3, weave_result, first_half, nc.scalar.copy, 0, 256)
-        at(slot + 0.4, scale_out, jobs[-2])
-        at(slot + 0.45, quantize_result, whole[-1])
+        at(slot + 0.35, scale_out, jobs[-2])
         at(slot + 0.5, scale_out, jobs[-1])
         at(slot + 0.6, quantize_result, first_half)
         at(slot + 0.7, weave_result, second_half, nc.scalar.copy, TAIL_COLS, 256)
         at(slot + 0.7, weave_result, second_half, nc.vector.tensor_copy, 0, TAIL_COLS)
         at(slot + 0.8, quantize_result, second_half)
-        at(slot + 0.9, store_scales, N - STRIP, N, [nc.scalar, nc.sync])
+        at(slot + 0.9, store_scales, 1, [nc.scalar, nc.sync])
 
         for slot, number, step, args in sorted(plan, key=lambda entry: entry[:2]):
             step(*args)

@@ -26,12 +26,12 @@ STRIPS = N // STRIP
 BANK = 512
 RUN = 4
 VECTOR_COLS_HEAD = 352
-VECTOR_COLS_MID = 256
+VECTOR_COLS_MID = 160
 VECTOR_COLS = 0
 POOL_COLS = 400
 TAIL_COLS = 160
 EARLY_GREEN = 10
-EARLY_UNITS = 3
+EARLY_UNITS = 4
 PER_ROUND = (2, 2, 2, 0, 0, 0, 0)
 Y_ROUND = (0, 0, 0, 2, 2, 2, 1)
 Y_COLS = 64
@@ -40,7 +40,14 @@ EXP_AT = 0.5
 Y_BUFS = 5
 SCALES_AT = 0.92
 STORE_SLOTS = 2
-POOL_LAST = 224
+POOL_LAST = 304
+POOL_MID = 112
+HALF_SLOTS = 4
+LATE_SHARE = 128
+POOL_END = 8
+SHARE_AT = 0.4
+VECTOR_COLS_NOPOOL = 256
+ARG_RATE = 2
 ARG_AT = 0.07
 QP = 0.52
 QG = 1.1
@@ -121,7 +128,7 @@ def tile_green_shot_response_g2_kernel(tc, pressure, green, absorption, path, lo
         codes = {}
         factors = {}
         y_tiles = {}
-        y_woven = {}
+        whole_tile = {}
         job_banks = {}
         passes_done = {}
 
@@ -150,12 +157,20 @@ def tile_green_shot_response_g2_kernel(tc, pressure, green, absorption, path, lo
         def fetch_gain(first, last):
             nc.vector.tensor_copy(out=gain_all[:].bitcast(F32)[:, first:last], in_=gain_bank[:, first:last])
 
+        def take_tile(things, name, bufs):
+            width = sum(PACK * (STRIP if thing[0] in ("shots", "green") else thing[2]) for thing in things)
+            tile = sbuf.tile([P, width], BF16, name=name, bufs=bufs, align_bytes=64)
+            whole_tile[things[0]] = tile
+            part = width // len(things)
+            for place, thing in enumerate(things):
+                woven[thing] = tile[:, place * part : (place + 1) * part]
+
         def woven_tile(item):
             if item not in woven:
                 if item in gated:
-                    woven[item] = sbuf.tile([P, K], BF16, name="gated", bufs=1, align_bytes=64)
+                    take_tile([item], "gated", 1)
                 else:
-                    woven[item] = sbuf.tile([P, K], BF16, name="woven", bufs=WOVEN_BUFS, align_bytes=64)
+                    take_tile([item], "woven", WOVEN_BUFS)
             return woven[item]
 
         def turn(item):
@@ -179,18 +194,21 @@ def tile_green_shot_response_g2_kernel(tc, pressure, green, absorption, path, lo
         def pool_weave(item, last):
             pool_interleave(woven_tile(item), raw[item], last)
 
-        def quantize(item):
-            count = len(shot_items) if item[0] == "shots" else len(green_items)
-            words = sbuf.tile([P, STRIP], U32, name=item[0] + "_codes", bufs=count, align_bytes=64)
-            scales = sbuf.tile([P, STRIP], U8, name=item[0] + "_scales", bufs=count, align_bytes=64)
-            nc.vector.quantize_mx(out=words[:].bitcast(FP8X4), scales=scales[:], in_=woven[item][:])
-            codes[item] = (words, scales)
+        def quantize(*items):
+            name = items[0][0] + "%d" % len(items)
+            count = len(shot_items) if items[0][0] == "shots" else (EARLY_GREEN if len(items) == 1 else len(late_items) // 2)
+            words = sbuf.tile([P, STRIP * len(items)], U32, name=name + "_codes", bufs=count, align_bytes=64)
+            scales = sbuf.tile([P, STRIP * len(items)], U8, name=name + "_scales", bufs=count, align_bytes=64)
+            nc.vector.quantize_mx(out=words[:].bitcast(FP8X4), scales=scales[:], in_=whole_tile[items[0]][:])
+            for place, item in enumerate(items):
+                cols = slice(place * STRIP, (place + 1) * STRIP)
+                codes[item] = (words[:, cols], scales[:, cols])
 
         def multiply(job, place, c):
             (g, col, width), slots = job
             if job not in job_banks:
                 index = jobs.index(job)
-                job_banks[job] = bank_tile(index % 4 if index < 8 else (index - 4) % 7)
+                job_banks[job] = bank_tile(index % 4 if index < 8 else (5, 6, 4, 0, 1, 2, 3)[(index - 8) % 7])
             n, first = divmod(col, STRIP)
             cols = slice(first, first + width)
             green_words, green_scales = codes[("green", n, c)]
@@ -213,24 +231,21 @@ def tile_green_shot_response_g2_kernel(tc, pressure, green, absorption, path, lo
                 for c in range(PASSES):
                     multiply(job, place, c)
 
-        def exponent(job):
-            unit, slots = job
-            g, col, width = unit
-            if unit not in factors:
-                factors[unit] = sbuf.tile([P, PACK, width // 2], F32, name="factor", bufs=EARLY_UNITS + 1)
-            receivers = slice(col // 2, (col + width) // 2)
-            for t in slots:
-                nc.vector.scalar_tensor_tensor(
-                    out=factors[unit][:, t, :],
-                    in0=path_bank[:].bitcast(BF16)[:, receivers],
-                    scalar=absorb[:, g, t : t + 1],
-                    in1=gain_all[:, receivers],
-                    op0=ALU.mult,
-                    op1=ALU.subtract,
-                )
+        def exponent(g, side, t):
+            if (g, side) not in factors:
+                factors[(g, side)] = sbuf.tile([P, PACK, R // 2], F32, name="factor", bufs=3)
+            receivers = slice(side * R // 2, (side + 1) * R // 2)
+            nc.vector.scalar_tensor_tensor(
+                out=factors[(g, side)][:, t, :],
+                in0=path_bank[:].bitcast(BF16)[:, receivers],
+                scalar=absorb[:, g, t : t + 1],
+                in1=gain_all[:, receivers],
+                op0=ALU.mult,
+                op1=ALU.subtract,
+            )
 
-        def exponential(unit, first, last):
-            part = factors[unit][:, first:last, :]
+        def exponential(g, side, first, last):
+            part = factors[(g, side)][:, first:last, :]
             nc.scalar.activation(out=part, in_=part, func=ACT.Exp, scale=-1.0)
 
         def scale_out(job):
@@ -239,36 +254,30 @@ def tile_green_shot_response_g2_kernel(tc, pressure, green, absorption, path, lo
             if unit not in y_tiles:
                 y_tiles[unit] = sbuf.tile([P, PACK, width], F32, name="y", bufs=Y_BUFS)
             ts = slice(slots[0], slots[-1] + 1)
+            side, first = divmod(col, N // 2)
             nc.vector.tensor_tensor(
                 out=y_tiles[unit][:, ts, :].rearrange("p t (r c) -> p t r c", c=2),
                 in0=job_banks[job][:].rearrange("p (t r c) -> p t r c", t=len(slots), c=2),
-                in1=factors[unit][:, ts, :].unsqueeze(3).to_broadcast([P, len(slots), width // 2, 2]),
+                in1=factors[(g, side)][:, ts, first // 2 : (first + width) // 2].unsqueeze(3).to_broadcast([P, len(slots), width // 2, 2]),
                 op=ALU.mult,
             )
-            if slots[-1] % STORE_SLOTS == STORE_SLOTS - 1:
-                pair = slice(slots[-1] + 1 - STORE_SLOTS, slots[-1] + 1)
+            count = STORE_SLOTS if unit in whole else HALF_SLOTS
+            if slots[-1] % count == count - 1:
+                pair = slice(slots[-1] + 1 - count, slots[-1] + 1)
                 nc.sync.dma_start(out=y_hbm[g, :, pair, col : col + width], in_=y_tiles[unit][:, pair, :])
 
-        def result_tile(unit):
-            if unit not in y_woven:
-                if unit in gated:
-                    y_woven[unit] = sbuf.tile([P, PACK * unit[2]], BF16, name="gated", bufs=1, align_bytes=64)
-                elif unit in whole:
-                    y_woven[unit] = sbuf.tile([P, PACK * unit[2]], BF16, name="y_woven", bufs=2, align_bytes=64)
-                else:
-                    y_woven[unit] = sbuf.tile([P, PACK * unit[2]], BF16, name="last_woven", bufs=2, align_bytes=64)
-            return y_woven[unit]
-
         def weave_result(unit, copy, first, last):
-            interleave(copy, result_tile(unit), y_tiles[unit], first, last)
+            interleave(copy, woven_tile(unit), y_tiles[unit], first, last)
 
         def pool_weave_result(unit, last):
-            pool_interleave(result_tile(unit), y_tiles[unit], last)
+            pool_interleave(woven_tile(unit), y_tiles[unit], last)
 
-        def quantize_result(unit):
-            g, col, width = unit
-            words = sbuf.tile([P, width], U32, name="y_codes", bufs=5, align_bytes=64)
-            nc.vector.quantize_mx(out=words[:].bitcast(FP8X4), scales=y_scales[col // (N // 2)][:, g, col % (N // 2) : col % (N // 2) + width], in_=y_woven[unit][:])
+        def quantize_result(*parts):
+            g, col, width = parts[0]
+            width = width * len(parts)
+            side, first = divmod(col, N // 2)
+            words = sbuf.tile([P, width], U32, name="y_codes", bufs=4, align_bytes=64)
+            nc.vector.quantize_mx(out=words[:].bitcast(FP8X4), scales=y_scales[side][:, g, first : first + width], in_=whole_tile[parts[0]][:])
             nc.sync.dma_start(out=words_hbm[g, :, col : col + width], in_=words[:].bitcast(I32))
 
         def store_scales(half, queues):
@@ -293,16 +302,13 @@ def tile_green_shot_response_g2_kernel(tc, pressure, green, absorption, path, lo
             at(5 + number / 2, load, item)
         at(-3, spread, gain_rows, gain_bank)
         at(-3, spread, path_rows, path_bank)
-        at(-3, fetch_gain, 0, P)
-        at(-2, exponent, jobs[0])
-        at(-2, exponent, jobs[1])
-        at(-2, exponential, units[0], 0, 2)
-        at(SPREAD_AT, fetch_gain, P, BANK)
-        for j, job in enumerate(jobs[2 : EARLY_UNITS * PACK]):
-            slot = 0.35 if j < 2 else (j + 0.35 if j < 6 else 6.35 + (j - 6) // ARGS_PER_BEAT)
-            at(slot, exponent, job)
-            if j % 2 and j + 2 < 2 * PACK:
-                at(slot + EXP_LAG, exponential, job[0], (j + 1) % PACK, (j + 1) % PACK + 2)
+        at(-3, fetch_gain, 0, BANK // 2)
+        at(SPREAD_AT, fetch_gain, BANK // 2, BANK)
+        for j in range(GROUPS * PACK):
+            g, t = divmod(j, PACK)
+            slot = (-2, 0.35)[j] if j < 2 else j + 0.35
+            at(slot, exponent, g, 0, t)
+            at(slot + (EXP_LAG if j else 0), exponential, g, 0, t, t + 1)
         quantized_at = {}
         for k, items in enumerate(beat_green):
             if k < len(shot_items):
@@ -312,9 +318,18 @@ def tile_green_shot_response_g2_kernel(tc, pressure, green, absorption, path, lo
                 at(k + 0.1, drain, shots, 1)
                 quantized_at[shots] = k + QP
             for number, item in enumerate(items):
-                share = VECTOR_COLS_HEAD if len(items) == 2 else VECTOR_COLS_MID
-                at(k + 0.2 + 0.3 * number, weave, item, nc.scalar.copy, share, STRIP)
-                at(k + 0.2 + 0.3 * number, weave, item, nc.vector.tensor_copy, 0, share)
+                if len(items) == 2:
+                    at(k + 0.2 + 0.3 * number, weave, item, nc.scalar.copy, VECTOR_COLS_HEAD, STRIP)
+                    at(k + 0.2 + 0.3 * number, weave, item, nc.vector.tensor_copy, 0, VECTOR_COLS_HEAD)
+                else:
+                    pm = POOL_MID if 2 < k < POOL_END else 0
+                    if POOL_MID:
+                        gated.append(item)
+                    if pm:
+                        at(k + 0.2, pool_weave, item, pm)
+                    share = VECTOR_COLS_MID if pm else VECTOR_COLS_NOPOOL
+                    at(k + 0.2, weave, item, nc.scalar.copy, pm + share, STRIP)
+                    at(k + SHARE_AT, weave, item, nc.vector.tensor_copy, pm, pm + share)
                 quantized_at[item] = k + (0.55 + 0.3 * number if len(items) == 2 else QG)
         quantized_at[gate_item] = len(shot_items) + 0.5
         for item in quantized_at:
@@ -326,39 +341,40 @@ def tile_green_shot_response_g2_kernel(tc, pressure, green, absorption, path, lo
             if g == 0:
                 at(WINDOW0 + t, scale_out, job)
 
-        taken = 0
-        finished = 0
+        pairs = [late_items[i : i + 2] for i in range(0, len(late_items), 2)]
+        pairs.extend([[units[0], units[2]], [units[1], units[3]]])
         for u in range(1, len(whole) + 1):
             slot = 30 + u
             for job in jobs[PACK * (u + 1) : PACK * (u + 2)]:
-                at(slot + 0.06, multiply_all, job)
+                at(7.51 if job == jobs[2 * PACK] else slot + 0.06, multiply_all, job)
             if u < len(whole):
                 for job in jobs[PACK * u : PACK * (u + 1)]:
                     at(slot + 0.05, scale_out, job)
-                for job in jobs[PACK * max(u + EARLY_UNITS - 1, EARLY_UNITS) : PACK * (u + EARLY_UNITS)]:
-                    at(slot + ARG_AT, exponent, job)
-                for unit in units[u + 1 : u + 2] if u + 1 < len(whole) else units[u + 1 :]:
-                    at(slot + EXP_AT, exponential, unit, 0, PACK)
-            work = []
-            for number in range(PER_ROUND[u - 1]):
-                work.append((late_items[taken], weave, pool_weave, quantize))
-                taken = taken + 1
-            for number in range(Y_ROUND[u - 1]):
-                work.append((units[finished], weave_result, pool_weave_result, quantize_result))
-                finished = finished + 1
-            for number, (what, by_copy, by_pool, finish) in enumerate(work):
-                if number == (min(PER_ROUND[u - 1], 2) - 1 if PER_ROUND[u - 1] else len(work) - 1):
-                    gated.append(what)
-                    pool_cols = POOL_COLS if u + 1 < len(whole) else POOL_LAST
-                    at(slot + 0.1, by_pool, what, pool_cols)
-                    if pool_cols < STRIP:
-                        at(slot + 0.1, by_copy, what, nc.scalar.copy, pool_cols, STRIP)
-                    at(slot + (0.9 if u < len(whole) else 0.55), finish, what)
-                else:
-                    at(slot + 0.11 + 0.1 * number, by_copy, what, nc.scalar.copy, VECTOR_COLS, STRIP)
-                    if VECTOR_COLS:
-                        at(slot + 0.3, by_copy, what, nc.vector.tensor_copy, 0, VECTOR_COLS)
-                    at(slot + 0.6 + 0.1 * number, finish, what)
+            if u <= 2 * GROUPS:
+                g, half = divmod(u - 1, 2)
+                at(slot + 0.07, exponent, g, 1, 2 * half)
+                at(slot + 0.07, exponent, g, 1, 2 * half + 1)
+                at(slot + 0.5, exponential, g, 1, 2 * half, 2 * half + 2)
+            pool_cols = POOL_COLS if u <= 2 * GROUPS else POOL_LAST
+            if u <= len(pairs):
+                first, second = pairs[u - 1]
+                by_copy, by_pool, finish = (weave, pool_weave, quantize) if first in late_items else (weave_result, pool_weave_result, quantize_result)
+                at(slot + 0.1, take_tile, pairs[u - 1], "gated", 1)
+                at(slot + 0.1, by_pool, first, pool_cols)
+                at(slot + 0.1, by_copy, first, nc.scalar.copy, pool_cols, STRIP)
+                share = 0 if u <= 2 * GROUPS else LATE_SHARE
+                at(slot + 0.1, by_copy, second, nc.scalar.copy, share, STRIP)
+                if share:
+                    at(slot + 0.2, by_copy, second, nc.vector.tensor_copy, 0, share)
+                at(slot + 0.9, finish, first, second)
+            else:
+                unit = units[u - 1]
+                gated.append(unit)
+                at(slot + 0.1, pool_weave_result, unit, pool_cols)
+                at(slot + 0.1, weave_result, unit, nc.scalar.copy, pool_cols, STRIP)
+                at(slot + (0.9 if u < len(whole) else 0.55), quantize_result, unit)
+        at(30 + len(pairs) + 0.6, weave_result, units[4], nc.scalar.copy, 0, STRIP)
+        at(30 + len(pairs) + 1.6, quantize_result, units[4])
         slot = 30 + len(whole)
         first_half, second_half = units[-2:]
         at(slot - SCALES_AT, store_scales, 0, [nc.sync])

@@ -23,114 +23,62 @@ PASSES = K // K_PASS
 GROUPS = S // K_PASS
 STRIP = 512
 STRIPS = N // STRIP
+SIDE = N // 2
 BANK = 512
 RUN = 4
-VECTOR_COLS_HEAD = 352
-VECTOR_COLS_MID = 160
-VECTOR_COLS = 0
-POOL_COLS = 400
-TAIL_COLS = 160
-EARLY_GREEN = 10
-EARLY_UNITS = 4
-PER_ROUND = (2, 2, 2, 0, 0, 0, 0)
-Y_ROUND = (0, 0, 0, 2, 2, 2, 1)
-Y_COLS = 64
-Y_LAG = 1.04
-EXP_AT = 0.5
-Y_BUFS = 5
-SCALES_AT = 0.92
-STORE_SLOTS = 2
-POOL_LAST = 304
-POOL_MID = 112
-HALF_SLOTS = 4
-LATE_SHARE = 128
-POOL_END = 8
-SHARE_AT = 0.4
-VECTOR_COLS_NOPOOL = 256
-ARG_RATE = 2
-ARG_AT = 0.07
-QP = 0.52
-QG = 1.1
-WINDOW0 = 2.3
-ARGS_PER_BEAT = 2
-ARG_SKIP = 1
-EXP_LAG = 0.5
-SPREAD_AT = 0.505
-TURN_LEAD = 0.49
-WOVEN_BUFS = 5
+
+TURN_BANKS = (4, 5, 6)
+JOB_BANKS = (5, 6, 4, 0, 1, 2, 3)
+GAIN_BANK = 1
+PATH_BANK = 7
+
+VECTOR_COLS_FIRST = 352
+VECTOR_COLS_HEAD = 160
+POOL_COLS_HEAD = 128
+POOL_COLS_SHORT = 304
+
+SCALE_LAG = 3
+LOAD_LEAD = 4
 
 
 def tile_green_shot_response_g2_kernel(tc, pressure, green, absorption, path, log_gain, out_0, out_1, out_2):
     nc = tc.nc
     green_kn = green.rearrange("k r c -> k (r c)")
+    shots_hbm = pressure.rearrange("(g p t) k -> g t p k", p=P, t=PACK)
     y_hbm = out_0.rearrange("(g p t) r c -> g p t (r c)", p=P, t=PACK)
     words_hbm = out_1.rearrange("g p m t -> g p (m t)").bitcast(I32)
     scales_hbm = out_2.bitcast(I32)
-    shots_hbm = pressure.rearrange("(g p t) k -> g t p k", p=P, t=PACK)
+
+    shot_tiles = [("shots", g, t) for g in range(GROUPS) for t in range(PACK)]
+    green_tiles = [("green", n, c) for n in range(STRIPS) for c in range(PASSES)]
+    beat_green = [green_tiles[:2], green_tiles[2:4]] + [[item] for item in green_tiles[4 : len(shot_tiles) + 2]]
+    late_green = green_tiles[len(shot_tiles) + 2 :]
+
+    units = [(g, n * STRIP, STRIP) for n in range(STRIPS) for g in range(GROUPS)]
+    last_g, last_col, last_width = units.pop()
+    halves = [(last_g, last_col + first, last_width // 2) for first in (0, last_width // 2)]
+    jobs = []
+    for unit in units + halves:
+        per_bank = BANK // unit[2]
+        jobs.extend((unit, tuple(range(t, t + per_bank))) for t in range(0, PACK, per_bank))
+    head_jobs = jobs[: GROUPS * PACK]
 
     with ExitStack() as ctx:
         sbuf = ctx.enter_context(tc.tile_pool(name="sbuf", bufs=1))
         psum = ctx.enter_context(tc.psum_pool(name="psum", bufs=1))
         ctx.enter_context(tc.manual_schedule())
 
-        def bank_tile(index):
-            return psum.tile([P, BANK], F32, name="bank%d" % index)
-
-        def interleave(copy, woven, rows, first, last):
-            copy(
-                out=woven[:, first * PACK : last * PACK].rearrange("p (c i t) -> p c t i", i=RUN, t=PACK),
-                in_=rows[:, :, first:last].rearrange("p t (c i) -> p c t i", i=RUN),
-            )
-
-        def pool_interleave(woven, rows, last):
-            nc.gpsimd.tensor_scalar(
-                out=woven[:, : last * PACK].rearrange("p (c t) -> p c t", t=PACK),
-                in0=rows[:, :, :last].rearrange("p t c -> p c t"),
-                scalar1=1.0,
-                scalar2=0.0,
-                op0=ALU.mult,
-                op1=ALU.add,
-            )
-
-        identity = sbuf.tile([P, P], F32, name="identity")
-        make_identity(nc, identity[:])
-
-        gain_rows = sbuf.tile([P, R // P], BF16, name="gain_rows")
-        nc.scalar.dma_start(out=gain_rows[:], in_=log_gain.rearrange("(p m) -> p m", p=P))
-        path_rows = sbuf.tile([P, R // P], BF16, name="path_rows")
-        nc.scalar.dma_start(out=path_rows[:], in_=path.rearrange("(p m) -> p m", p=P))
-        absorb = sbuf.tile([P, GROUPS, PACK], BF16, name="absorb")
-        nc.scalar.dma_start(out=absorb[:], in_=absorption.rearrange("(g p t) -> p g t", p=P, t=PACK))
-        early_scales = sbuf.tile([P, GROUPS, N // 2], U8, name="early_scales", align_bytes=64)
-        late_scales = sbuf.tile([P, GROUPS, N // 2], U8, name="late_scales", align_bytes=64)
-        y_scales = (early_scales, late_scales)
-
-        shot_items = [("shots", g, t) for g in range(GROUPS) for t in range(PACK)]
-        green_items = [("green", n, c) for n in range(STRIPS) for c in range(PASSES)]
-        beat_green = [green_items[:2], green_items[2:4]] + [[item] for item in green_items[4:EARLY_GREEN]]
-        late_items = green_items[EARLY_GREEN:]
-        gate_item = green_items[EARLY_GREEN - 1]
-
-        units = [(g, n * STRIP, STRIP) for n in range(STRIPS) for g in range(GROUPS)]
-        last_g, last_col, last_width = units.pop()
-        whole = list(units)
-        units.extend([(last_g, last_col, last_width // 2), (last_g, last_col + last_width // 2, last_width // 2)])
-        jobs = []
-        for unit in units:
-            per_bank = BANK // unit[2]
-            for t0 in range(0, PACK, per_bank):
-                jobs.append((unit, tuple(range(t0, t0 + per_bank))))
-
-        gated = [gate_item]
         raw = {}
         woven = {}
-        turned = {}
+        woven_whole = {}
+        turned = []
         codes = {}
         factors = {}
-        y_tiles = {}
-        whole_tile = {}
         job_banks = {}
         passes_done = {}
+
+        def bank_tile(index):
+            return psum.tile([P, BANK], F32, name="bank%d" % index)
 
         def load(item):
             kind, a, b = item
@@ -140,66 +88,67 @@ def tile_green_shot_response_g2_kernel(tc, pressure, green, absorption, path, lo
             else:
                 tile = sbuf.tile([P, PACK, STRIP], BF16, name="green_raw", bufs=8)
                 rows = green_kn[b * K_PASS : (b + 1) * K_PASS, a * STRIP : (a + 1) * STRIP]
-                nc.sync.dma_start(out=tile[:], in_=rows.rearrange("(p j) w -> p j w", j=PACK))
+                nc.sync.dma_start(out=tile[:], in_=rows.rearrange("(p t) w -> p t w", t=PACK))
             raw[item] = tile
-
-        path_bank = bank_tile(7)
-        gain_all = sbuf.tile([P, R], BF16, name="gain_all")
-
-        gain_bank = bank_tile(1)
 
         def spread(rows, bank):
             words = rows[:].bitcast(F32)
-            count = R // P // 2
+            count = words.shape[1]
             for m in range(count):
                 nc.tensor.transpose(bank[:, m::count], words[:, m : m + 1].to_broadcast([P, P]), identity[:])
 
-        def fetch_gain(first, last):
-            nc.vector.tensor_copy(out=gain_all[:].bitcast(F32)[:, first:last], in_=gain_bank[:, first:last])
+        def fetch_gain(side):
+            words = slice(side * BANK // 2, (side + 1) * BANK // 2)
+            nc.vector.tensor_copy(out=gain_all[:].bitcast(F32)[:, words], in_=gain_bank[:, words])
 
-        def take_tile(things, name, bufs):
-            width = sum(PACK * (STRIP if thing[0] in ("shots", "green") else thing[2]) for thing in things)
-            tile = sbuf.tile([P, width], BF16, name=name, bufs=bufs, align_bytes=64)
-            whole_tile[things[0]] = tile
-            part = width // len(things)
+        def take_woven(things, width, name, bufs):
+            tile = sbuf.tile([P, len(things) * PACK * width], BF16, name=name, bufs=bufs, align_bytes=64)
+            woven_whole[things[0]] = tile
             for place, thing in enumerate(things):
-                woven[thing] = tile[:, place * part : (place + 1) * part]
+                woven[thing] = tile[:, place * PACK * width : (place + 1) * PACK * width]
 
-        def woven_tile(item):
-            if item not in woven:
-                if item in gated:
-                    take_tile([item], "gated", 1)
-                else:
-                    take_tile([item], "woven", WOVEN_BUFS)
-            return woven[item]
+        def take_free(thing, width):
+            take_woven([thing], width, "woven", 5)
+
+        def take_gated(things):
+            take_woven(things, STRIP, "gated", 1)
 
         def turn(item):
             words = raw[item][:].bitcast(F32)
             for half in range(2):
-                bank = bank_tile(4 + len(turned) % 3)
+                bank = bank_tile(TURN_BANKS[len(turned) % len(TURN_BANKS)])
                 for j in range(4):
                     first = 256 * (2 * half + j // 2) + j % 2
                     nc.tensor.transpose(bank[:, j * P : (j + 1) * P], words[:, first : first + 255 : 2], identity[:])
-                turned[(item, half)] = bank
+                turned.append(bank)
 
-        def drain(item, half):
-            nc.scalar.copy(
-                out=woven_tile(item)[:, half * 1024 : (half + 1) * 1024].bitcast(F32).rearrange("p (c m u) -> p c m u", c=2, u=2),
-                in_=turned[(item, half)][:].rearrange("p (c u m) -> p c m u", c=2, u=2),
+        def drain(item):
+            take_free(item, STRIP)
+            words = woven[item].bitcast(F32).rearrange("p (h c m u) -> p h c m u", h=2, c=2, u=2)
+            for half, bank in enumerate(turned[-2:]):
+                nc.scalar.copy(out=words[:, half], in_=bank[:].rearrange("p (c u m) -> p c m u", c=2, u=2))
+
+        def weave(thing, copy, first, last):
+            copy(
+                out=woven[thing][:, first * PACK : last * PACK].rearrange("p (c i t) -> p c t i", i=RUN, t=PACK),
+                in_=raw[thing][:, :, first:last].rearrange("p t (c i) -> p c t i", i=RUN),
             )
 
-        def weave(item, copy, first, last):
-            interleave(copy, woven_tile(item), raw[item], first, last)
+        def pool_weave(thing, last):
+            nc.gpsimd.tensor_scalar(
+                out=woven[thing][:, : last * PACK].rearrange("p (c t) -> p c t", t=PACK),
+                in0=raw[thing][:, :, :last].rearrange("p t c -> p c t"),
+                scalar1=1.0,
+                scalar2=0.0,
+                op0=ALU.mult,
+                op1=ALU.add,
+            )
 
-        def pool_weave(item, last):
-            pool_interleave(woven_tile(item), raw[item], last)
-
-        def quantize(*items):
+        def quantize(items, bufs):
             name = items[0][0] + "%d" % len(items)
-            count = len(shot_items) if items[0][0] == "shots" else (EARLY_GREEN if len(items) == 1 else len(late_items) // 2)
-            words = sbuf.tile([P, STRIP * len(items)], U32, name=name + "_codes", bufs=count, align_bytes=64)
-            scales = sbuf.tile([P, STRIP * len(items)], U8, name=name + "_scales", bufs=count, align_bytes=64)
-            nc.vector.quantize_mx(out=words[:].bitcast(FP8X4), scales=scales[:], in_=whole_tile[items[0]][:])
+            words = sbuf.tile([P, STRIP * len(items)], U32, name=name + "_codes", bufs=bufs, align_bytes=64)
+            scales = sbuf.tile([P, STRIP * len(items)], U8, name=name + "_scales", bufs=bufs, align_bytes=64)
+            nc.vector.quantize_mx(out=words[:].bitcast(FP8X4), scales=scales[:], in_=woven_whole[items[0]][:])
             for place, item in enumerate(items):
                 cols = slice(place * STRIP, (place + 1) * STRIP)
                 codes[item] = (words[:, cols], scales[:, cols])
@@ -208,7 +157,8 @@ def tile_green_shot_response_g2_kernel(tc, pressure, green, absorption, path, lo
             (g, col, width), slots = job
             if job not in job_banks:
                 index = jobs.index(job)
-                job_banks[job] = bank_tile(index % 4 if index < 8 else (5, 6, 4, 0, 1, 2, 3)[(index - 8) % 7])
+                late = index - len(head_jobs)
+                job_banks[job] = bank_tile(index % PACK if late < 0 else JOB_BANKS[late % len(JOB_BANKS)])
             n, first = divmod(col, STRIP)
             cols = slice(first, first + width)
             green_words, green_scales = codes[("green", n, c)]
@@ -231,6 +181,14 @@ def tile_green_shot_response_g2_kernel(tc, pressure, green, absorption, path, lo
                 for c in range(PASSES):
                     multiply(job, place, c)
 
+        def quantize_and_multiply(item):
+            quantize([item], len(shot_tiles) if item in shot_tiles else len(green_tiles) - len(late_green))
+            for job, shots in zip(head_jobs, shot_tiles):
+                for c in range(PASSES):
+                    needs = (shots, green_tiles[c])
+                    if item in needs and all(need in codes for need in needs):
+                        multiply(job, 0, c)
+
         def exponent(g, side, t):
             if (g, side) not in factors:
                 factors[(g, side)] = sbuf.tile([P, PACK, R // 2], F32, name="factor", bufs=3)
@@ -251,143 +209,158 @@ def tile_green_shot_response_g2_kernel(tc, pressure, green, absorption, path, lo
         def scale_out(job):
             unit, slots = job
             g, col, width = unit
-            if unit not in y_tiles:
-                y_tiles[unit] = sbuf.tile([P, PACK, width], F32, name="y", bufs=Y_BUFS)
+            if unit not in raw:
+                raw[unit] = sbuf.tile([P, PACK, width], F32, name="y", bufs=5)
             ts = slice(slots[0], slots[-1] + 1)
-            side, first = divmod(col, N // 2)
+            side, first = divmod(col, SIDE)
+            factor = factors[(g, side)][:, ts, first // 2 : (first + width) // 2]
             nc.vector.tensor_tensor(
-                out=y_tiles[unit][:, ts, :].rearrange("p t (r c) -> p t r c", c=2),
+                out=raw[unit][:, ts, :].rearrange("p t (r c) -> p t r c", c=2),
                 in0=job_banks[job][:].rearrange("p (t r c) -> p t r c", t=len(slots), c=2),
-                in1=factors[(g, side)][:, ts, first // 2 : (first + width) // 2].unsqueeze(3).to_broadcast([P, len(slots), width // 2, 2]),
+                in1=factor.unsqueeze(3).to_broadcast([P, len(slots), width // 2, 2]),
                 op=ALU.mult,
             )
-            count = STORE_SLOTS if unit in whole else HALF_SLOTS
+            count = PACK if unit in halves else 2
             if slots[-1] % count == count - 1:
-                pair = slice(slots[-1] + 1 - count, slots[-1] + 1)
-                nc.sync.dma_start(out=y_hbm[g, :, pair, col : col + width], in_=y_tiles[unit][:, pair, :])
+                stored = slice(slots[-1] + 1 - count, slots[-1] + 1)
+                nc.sync.dma_start(out=y_hbm[g, :, stored, col : col + width], in_=raw[unit][:, stored, :])
 
-        def weave_result(unit, copy, first, last):
-            interleave(copy, woven_tile(unit), y_tiles[unit], first, last)
-
-        def pool_weave_result(unit, last):
-            pool_interleave(woven_tile(unit), y_tiles[unit], last)
-
-        def quantize_result(*parts):
+        def quantize_result(parts):
             g, col, width = parts[0]
             width = width * len(parts)
-            side, first = divmod(col, N // 2)
+            side, first = divmod(col, SIDE)
             words = sbuf.tile([P, width], U32, name="y_codes", bufs=4, align_bytes=64)
-            nc.vector.quantize_mx(out=words[:].bitcast(FP8X4), scales=y_scales[side][:, g, first : first + width], in_=whole_tile[parts[0]][:])
+            scales = y_scales[side][:, g, first : first + width]
+            nc.vector.quantize_mx(out=words[:].bitcast(FP8X4), scales=scales, in_=woven_whole[parts[0]][:])
             nc.sync.dma_start(out=words_hbm[g, :, col : col + width], in_=words[:].bitcast(I32))
 
-        def store_scales(half, queues):
-            first = half * N // 2
-            last = first + N // 2
+        def store_scales(side, queues):
+            words = slice(side * SIDE // 4, (side + 1) * SIDE // 4)
             for q in range(4):
                 queues[q % len(queues)].dma_start(
-                    out=scales_hbm[:, 4 * q : 4 * q + 4, first // 4 : last // 4].rearrange("g r m -> r g m"),
-                    in_=y_scales[half][32 * q : 32 * q + 4].bitcast(I32),
+                    out=scales_hbm[:, 4 * q : 4 * q + 4, words].rearrange("g r m -> r g m"),
+                    in_=y_scales[side][32 * q : 32 * q + 4].bitcast(I32),
                 )
 
-        plan = []
+        identity = sbuf.tile([P, P], F32, name="identity")
+        make_identity(nc, identity[:])
+        gain_rows = sbuf.tile([P, R // P], BF16, name="gain_rows")
+        nc.scalar.dma_start(out=gain_rows[:], in_=log_gain.rearrange("(p m) -> p m", p=P))
+        path_rows = sbuf.tile([P, R // P], BF16, name="path_rows")
+        nc.scalar.dma_start(out=path_rows[:], in_=path.rearrange("(p m) -> p m", p=P))
+        absorb = sbuf.tile([P, GROUPS, PACK], BF16, name="absorb")
+        nc.scalar.dma_start(out=absorb[:], in_=absorption.rearrange("(g p t) -> p g t", p=P, t=PACK))
+        early_scales = sbuf.tile([P, GROUPS, SIDE], U8, name="early_scales", align_bytes=64)
+        late_scales = sbuf.tile([P, GROUPS, SIDE], U8, name="late_scales", align_bytes=64)
+        y_scales = (early_scales, late_scales)
 
-        def at(slot, step, *args):
-            plan.append((slot, len(plan), step, args))
+        beat_loads = [[shots] + items for shots, items in zip(shot_tiles, beat_green)]
+        for items in beat_loads[:LOAD_LEAD]:
+            for item in items:
+                load(item)
+        beat_loads = beat_loads[LOAD_LEAD:] + [[]] + [late_green[i : i + 2] for i in range(0, len(late_green), 2)]
 
-        beat_green = beat_green[:-1] + [[]] * (len(shot_items) - len(beat_green)) + beat_green[-1:]
-        for k, shots in enumerate(shot_items):
-            for item in [shots] + beat_green[k]:
-                at(k - 4, load, item)
-        for number, item in enumerate(late_items):
-            at(5 + number / 2, load, item)
-        at(-3, spread, gain_rows, gain_bank)
-        at(-3, spread, path_rows, path_bank)
-        at(-3, fetch_gain, 0, BANK // 2)
-        at(SPREAD_AT, fetch_gain, BANK // 2, BANK)
-        for j in range(GROUPS * PACK):
-            g, t = divmod(j, PACK)
-            slot = (-2, 0.35)[j] if j < 2 else j + 0.35
-            at(slot, exponent, g, 0, t)
-            at(slot + (EXP_LAG if j else 0), exponential, g, 0, t, t + 1)
-        quantized_at = {}
-        for k, items in enumerate(beat_green):
-            if k < len(shot_items):
-                shots = shot_items[k]
-                at(k - TURN_LEAD, turn, shots)
-                at(k + 0.1, drain, shots, 0)
-                at(k + 0.1, drain, shots, 1)
-                quantized_at[shots] = k + QP
-            for number, item in enumerate(items):
-                if len(items) == 2:
-                    at(k + 0.2 + 0.3 * number, weave, item, nc.scalar.copy, VECTOR_COLS_HEAD, STRIP)
-                    at(k + 0.2 + 0.3 * number, weave, item, nc.vector.tensor_copy, 0, VECTOR_COLS_HEAD)
-                else:
-                    pm = POOL_MID if 2 < k < POOL_END else 0
-                    if POOL_MID:
-                        gated.append(item)
-                    if pm:
-                        at(k + 0.2, pool_weave, item, pm)
-                    share = VECTOR_COLS_MID if pm else VECTOR_COLS_NOPOOL
-                    at(k + 0.2, weave, item, nc.scalar.copy, pm + share, STRIP)
-                    at(k + SHARE_AT, weave, item, nc.vector.tensor_copy, pm, pm + share)
-                quantized_at[item] = k + (0.55 + 0.3 * number if len(items) == 2 else QG)
-        quantized_at[gate_item] = len(shot_items) + 0.5
-        for item in quantized_at:
-            at(quantized_at[item], quantize, item)
-        for j, job in enumerate(jobs[: 2 * PACK]):
-            g, t = divmod(j, PACK)
-            for c in range(PASSES):
-                at(max(quantized_at[("shots", g, t)], quantized_at[("green", 0, c)]) + 0.01, multiply, job, 0, c)
-            if g == 0:
-                at(WINDOW0 + t, scale_out, job)
+        path_bank = bank_tile(PATH_BANK)
+        gain_bank = bank_tile(GAIN_BANK)
+        gain_all = sbuf.tile([P, R], BF16, name="gain_all")
+        spread(gain_rows, gain_bank)
+        spread(path_rows, path_bank)
+        fetch_gain(0)
+        exponent(0, 0, 0)
+        exponential(0, 0, 0, 1)
+        turn(shot_tiles[0])
 
-        pairs = [late_items[i : i + 2] for i in range(0, len(late_items), 2)]
-        pairs.extend([[units[0], units[2]], [units[1], units[3]]])
-        for u in range(1, len(whole) + 1):
-            slot = 30 + u
-            for job in jobs[PACK * (u + 1) : PACK * (u + 2)]:
-                at(7.51 if job == jobs[2 * PACK] else slot + 0.06, multiply_all, job)
-            if u < len(whole):
-                for job in jobs[PACK * u : PACK * (u + 1)]:
-                    at(slot + 0.05, scale_out, job)
-            if u <= 2 * GROUPS:
-                g, half = divmod(u - 1, 2)
-                at(slot + 0.07, exponent, g, 1, 2 * half)
-                at(slot + 0.07, exponent, g, 1, 2 * half + 1)
-                at(slot + 0.5, exponential, g, 1, 2 * half, 2 * half + 2)
-            pool_cols = POOL_COLS if u <= 2 * GROUPS else POOL_LAST
-            if u <= len(pairs):
-                first, second = pairs[u - 1]
-                by_copy, by_pool, finish = (weave, pool_weave, quantize) if first in late_items else (weave_result, pool_weave_result, quantize_result)
-                at(slot + 0.1, take_tile, pairs[u - 1], "gated", 1)
-                at(slot + 0.1, by_pool, first, pool_cols)
-                at(slot + 0.1, by_copy, first, nc.scalar.copy, pool_cols, STRIP)
-                share = 0 if u <= 2 * GROUPS else LATE_SHARE
-                at(slot + 0.1, by_copy, second, nc.scalar.copy, share, STRIP)
-                if share:
-                    at(slot + 0.2, by_copy, second, nc.vector.tensor_copy, 0, share)
-                at(slot + 0.9, finish, first, second)
+        for k, shots in enumerate(shot_tiles):
+            for item in beat_loads[k]:
+                load(item)
+            drain(shots)
+            items = beat_green[k]
+            if len(items) == 2:
+                for item in items:
+                    take_free(item, STRIP)
+                    weave(item, nc.scalar.copy, VECTOR_COLS_FIRST, STRIP)
+                    weave(item, nc.vector.tensor_copy, 0, VECTOR_COLS_FIRST)
+                    if item == green_tiles[0]:
+                        exponent(0, 0, 1)
+                if k == 0:
+                    fetch_gain(1)
+                turn(shot_tiles[k + 1])
+                quantize_and_multiply(shots)
+                for item in items:
+                    quantize_and_multiply(item)
+                if k == 0:
+                    exponential(0, 0, 1, 2)
+                continue
+            follows_gated = len(beat_green[k - 1]) == 1
+            if follows_gated:
+                quantize_and_multiply(beat_green[k - 1][0])
+            take_gated(items)
+            if follows_gated:
+                pool_weave(items[0], POOL_COLS_HEAD)
+            weave(items[0], nc.scalar.copy, POOL_COLS_HEAD + VECTOR_COLS_HEAD, STRIP)
+            if 0 <= k - SCALE_LAG < PACK:
+                scale_out(jobs[k - SCALE_LAG])
+            g, t = divmod(k, PACK)
+            exponent(g, 0, t)
+            weave(items[0], nc.vector.tensor_copy, POOL_COLS_HEAD if follows_gated else 0, POOL_COLS_HEAD + VECTOR_COLS_HEAD)
+            if k + 1 < len(shot_tiles):
+                turn(shot_tiles[k + 1])
             else:
-                unit = units[u - 1]
-                gated.append(unit)
-                at(slot + 0.1, pool_weave_result, unit, pool_cols)
-                at(slot + 0.1, weave_result, unit, nc.scalar.copy, pool_cols, STRIP)
-                at(slot + (0.9 if u < len(whole) else 0.55), quantize_result, unit)
-        at(30 + len(pairs) + 0.6, weave_result, units[4], nc.scalar.copy, 0, STRIP)
-        at(30 + len(pairs) + 1.6, quantize_result, units[4])
-        slot = 30 + len(whole)
-        first_half, second_half = units[-2:]
-        at(slot - SCALES_AT, store_scales, 0, [nc.sync])
-        at(slot + 0.05, scale_out, jobs[-4])
-        at(slot + 0.05, scale_out, jobs[-3])
-        at(slot + 0.3, weave_result, first_half, nc.scalar.copy, 0, 256)
-        at(slot + 0.35, scale_out, jobs[-2])
-        at(slot + 0.5, scale_out, jobs[-1])
-        at(slot + 0.6, quantize_result, first_half)
-        at(slot + 0.7, weave_result, second_half, nc.scalar.copy, TAIL_COLS, 256)
-        at(slot + 0.7, weave_result, second_half, nc.vector.tensor_copy, 0, TAIL_COLS)
-        at(slot + 0.8, quantize_result, second_half)
-        at(slot + 0.9, store_scales, 1, [nc.scalar, nc.sync])
+                multiply_all(jobs[len(head_jobs)])
+            quantize_and_multiply(shots)
+            exponential(g, 0, t, t + 1)
+        quantize_and_multiply(beat_green[-1][0])
 
-        for slot, number, step, args in sorted(plan, key=lambda entry: entry[:2]):
-            step(*args)
+        pairs = [late_green[i : i + 2] for i in range(0, len(late_green), 2)] + [[units[1], units[1 + GROUPS]]]
+        for u in range(1, len(units)):
+            for job in jobs[PACK * u : PACK * (u + 1)]:
+                scale_out(job)
+            for job in jobs[PACK * (u + 1) : PACK * (u + 2)]:
+                if job not in job_banks:
+                    multiply_all(job)
+            if u <= len(pairs):
+                g, t = divmod(2 * (u - 1), PACK)
+                exponent(g, 1, t)
+                exponent(g, 1, t + 1)
+                strip, half = divmod(u - 1, 2)
+                halved = units[GROUPS * strip]
+                if half == 0:
+                    take_free(halved, STRIP)
+                weave(halved, nc.scalar.copy, half * STRIP // 2, (half + 1) * STRIP // 2)
+                first, second = pairs[u - 1]
+                take_gated(pairs[u - 1])
+                pool_weave(first, STRIP)
+                weave(second, nc.scalar.copy, 0, STRIP)
+                exponential(g, 1, t, t + 2)
+                if half == 1:
+                    quantize_result([halved])
+                if first in late_green:
+                    quantize(pairs[u - 1], len(late_green) // 2)
+                else:
+                    quantize_result(pairs[u - 1])
+            else:
+                take_gated([units[u - 1]])
+                pool_weave(units[u - 1], POOL_COLS_SHORT)
+                weave(units[u - 1], nc.scalar.copy, POOL_COLS_SHORT, STRIP)
+                if u == len(pairs) + 1:
+                    store_scales(0, [nc.sync])
+                quantize_result([units[u - 1]])
+
+        first_half, second_half = halves
+        width = first_half[2]
+        for job in jobs[-4:-2]:
+            scale_out(job)
+        take_gated([units[-1]])
+        pool_weave(units[-1], POOL_COLS_SHORT)
+        weave(units[-1], nc.scalar.copy, POOL_COLS_SHORT, STRIP)
+        take_free(first_half, width)
+        weave(first_half, nc.scalar.copy, 0, width)
+        for job in jobs[-2:]:
+            scale_out(job)
+        quantize_result([units[-1]])
+        quantize_result([first_half])
+        take_free(second_half, width)
+        weave(second_half, nc.scalar.copy, VECTOR_COLS_HEAD, width)
+        weave(second_half, nc.vector.tensor_copy, 0, VECTOR_COLS_HEAD)
+        quantize_result([second_half])
+        store_scales(1, [nc.scalar, nc.sync])

@@ -34,6 +34,7 @@ PATH_BANK = 7
 
 VECTOR_COLS_FIRST = 352
 VECTOR_COLS_HEAD = 160
+VECTOR_COLS_LAST = 96
 POOL_COLS_HEAD = 128
 POOL_COLS_SHORT = 304
 
@@ -230,7 +231,7 @@ def tile_green_shot_response_g2_kernel(tc, pressure, green, absorption, path, lo
             width = width * len(parts)
             side, first = divmod(col, SIDE)
             words = sbuf.tile([P, width], U32, name="y_codes", bufs=4, align_bytes=64)
-            scales = y_scales[side][:, g, first : first + width]
+            scales = y_scales[side][4 * g :, first : first + width]
             nc.vector.quantize_mx(out=words[:].bitcast(FP8X4), scales=scales, in_=woven_whole[parts[0]][:])
             nc.sync.dma_start(out=words_hbm[g, :, col : col + width], in_=words[:].bitcast(I32))
 
@@ -238,8 +239,8 @@ def tile_green_shot_response_g2_kernel(tc, pressure, green, absorption, path, lo
             words = slice(side * SIDE // 4, (side + 1) * SIDE // 4)
             for q in range(4):
                 queues[q % len(queues)].dma_start(
-                    out=scales_hbm[:, 4 * q : 4 * q + 4, words].rearrange("g r m -> r g m"),
-                    in_=y_scales[side][32 * q : 32 * q + 4].bitcast(I32),
+                    out=scales_hbm[:, 4 * q : 4 * q + 4, words],
+                    in_=y_scales[side][32 * q : 32 * q + 4 * GROUPS].bitcast(I32),
                 )
 
         identity = sbuf.tile([P, P], F32, name="identity")
@@ -250,8 +251,8 @@ def tile_green_shot_response_g2_kernel(tc, pressure, green, absorption, path, lo
         nc.scalar.dma_start(out=path_rows[:], in_=path.rearrange("(p m) -> p m", p=P))
         absorb = sbuf.tile([P, GROUPS, PACK], BF16, name="absorb")
         nc.scalar.dma_start(out=absorb[:], in_=absorption.rearrange("(g p t) -> p g t", p=P, t=PACK))
-        early_scales = sbuf.tile([P, GROUPS, SIDE], U8, name="early_scales", align_bytes=64)
-        late_scales = sbuf.tile([P, GROUPS, SIDE], U8, name="late_scales", align_bytes=64)
+        early_scales = sbuf.tile([P, SIDE], U8, name="early_scales", align_bytes=64)
+        late_scales = sbuf.tile([P, SIDE], U8, name="late_scales", align_bytes=64)
         y_scales = (early_scales, late_scales)
 
         beat_loads = [[shots] + items for shots, items in zip(shot_tiles, beat_green)]
@@ -291,18 +292,18 @@ def tile_green_shot_response_g2_kernel(tc, pressure, green, absorption, path, lo
                 if k == 0:
                     exponential(0, 0, 1, 2)
                 continue
-            follows_gated = len(beat_green[k - 1]) == 1
-            if follows_gated:
+            if len(beat_green[k - 1]) == 1:
                 quantize_and_multiply(beat_green[k - 1][0])
             take_gated(items)
-            if follows_gated:
+            with_product = 0 <= k - SCALE_LAG < PACK
+            if with_product:
                 pool_weave(items[0], POOL_COLS_HEAD)
             weave(items[0], nc.scalar.copy, POOL_COLS_HEAD + VECTOR_COLS_HEAD, STRIP)
-            if 0 <= k - SCALE_LAG < PACK:
+            if with_product:
                 scale_out(jobs[k - SCALE_LAG])
             g, t = divmod(k, PACK)
             exponent(g, 0, t)
-            weave(items[0], nc.vector.tensor_copy, POOL_COLS_HEAD if follows_gated else 0, POOL_COLS_HEAD + VECTOR_COLS_HEAD)
+            weave(items[0], nc.vector.tensor_copy, POOL_COLS_HEAD if with_product else 0, POOL_COLS_HEAD + VECTOR_COLS_HEAD)
             if k + 1 < len(shot_tiles):
                 turn(shot_tiles[k + 1])
             else:
@@ -311,7 +312,7 @@ def tile_green_shot_response_g2_kernel(tc, pressure, green, absorption, path, lo
             exponential(g, 0, t, t + 1)
         quantize_and_multiply(beat_green[-1][0])
 
-        pairs = [late_green[i : i + 2] for i in range(0, len(late_green), 2)] + [[units[1], units[1 + GROUPS]]]
+        pairs = [late_green[i : i + 2] for i in range(0, len(late_green), 2)] + [[units[0], units[GROUPS]]]
         for u in range(1, len(units)):
             for job in jobs[PACK * u : PACK * (u + 1)]:
                 scale_out(job)
@@ -322,29 +323,31 @@ def tile_green_shot_response_g2_kernel(tc, pressure, green, absorption, path, lo
                 g, t = divmod(2 * (u - 1), PACK)
                 exponent(g, 1, t)
                 exponent(g, 1, t + 1)
-                strip, half = divmod(u - 1, 2)
-                halved = units[GROUPS * strip]
+            strip, half = divmod(u - 2, 2)
+            halved = units[GROUPS * strip + 1] if 0 <= strip < 2 else None
+            if halved:
                 if half == 0:
                     take_free(halved, STRIP)
                 weave(halved, nc.scalar.copy, half * STRIP // 2, (half + 1) * STRIP // 2)
-                first, second = pairs[u - 1]
-                take_gated(pairs[u - 1])
-                pool_weave(first, STRIP)
-                weave(second, nc.scalar.copy, 0, STRIP)
+            if u <= len(pairs):
+                gated = pairs[u - 1]
+                take_gated(gated)
+                pool_weave(gated[0], STRIP)
+                weave(gated[1], nc.scalar.copy, 0, STRIP)
                 exponential(g, 1, t, t + 2)
-                if half == 1:
-                    quantize_result([halved])
-                if first in late_green:
-                    quantize(pairs[u - 1], len(late_green) // 2)
-                else:
-                    quantize_result(pairs[u - 1])
             else:
-                take_gated([units[u - 1]])
-                pool_weave(units[u - 1], POOL_COLS_SHORT)
-                weave(units[u - 1], nc.scalar.copy, POOL_COLS_SHORT, STRIP)
-                if u == len(pairs) + 1:
+                gated = [units[u - 1]]
+                take_gated(gated)
+                pool_weave(gated[0], POOL_COLS_SHORT)
+                weave(gated[0], nc.scalar.copy, POOL_COLS_SHORT, STRIP)
+            if halved and half == 1:
+                quantize_result([halved])
+                if strip == 1:
                     store_scales(0, [nc.sync])
-                quantize_result([units[u - 1]])
+            if gated[0] in late_green:
+                quantize(gated, len(late_green) // 2)
+            else:
+                quantize_result(gated)
 
         first_half, second_half = halves
         width = first_half[2]
@@ -360,7 +363,7 @@ def tile_green_shot_response_g2_kernel(tc, pressure, green, absorption, path, lo
         quantize_result([units[-1]])
         quantize_result([first_half])
         take_free(second_half, width)
-        weave(second_half, nc.scalar.copy, VECTOR_COLS_HEAD, width)
-        weave(second_half, nc.vector.tensor_copy, 0, VECTOR_COLS_HEAD)
+        weave(second_half, nc.scalar.copy, VECTOR_COLS_LAST, width)
+        weave(second_half, nc.vector.tensor_copy, 0, VECTOR_COLS_LAST)
         quantize_result([second_half])
         store_scales(1, [nc.scalar, nc.sync])

from contextlib import ExitStack

import concourse.mybir as mybir
from concourse.masks import make_identity

S, K, R = 1024, 2048, 1024
N = 2 * R
FLOPS = 2 * S * K * N

F32 = mybir.dt.float32
BF16 = mybir.dt.bfloat16
I32 = mybir.dt.int32
U32 = mybir.dt.uint32
U8 = mybir.dt.uint8
FP8X4 = mybir.dt.float8_e4m3fn_x4
ALU = mybir.AluOpType
ACT = mybir.ActivationFunctionType

P = 128
PACK = 4
K_PASS = P * PACK
PASSES = K // K_PASS
GROUPS = S // K_PASS
STRIP = 512
STRIPS = N // STRIP
SIDE = N // 2
BANK = 512
RUN = 4

TURN_BANKS = (4, 5, 6)
JOB_BANKS = (5, 6, 4, 0, 1, 2, 3)
GAIN_BANK = 1
PATH_BANK = 7

VECTOR_COLS_FIRST = 352
VECTOR_COLS_HEAD = 160
VECTOR_COLS_LAST = 96
POOL_COLS_HEAD = 128
POOL_COLS_SHORT = 304

SCALE_LAG = 3
LOAD_LEAD = 4


def tile_green_shot_response_g2_kernel(tc, pressure, green, absorption, path, log_gain, out_0, out_1, out_2):
    nc = tc.nc
    green_kn = green.rearrange("k r c -> k (r c)")
    shots_hbm = pressure.rearrange("(g p t) k -> g t p k", p=P, t=PACK)
    y_hbm = out_0.rearrange("(g p t) r c -> g p t (r c)", p=P, t=PACK)
    words_hbm = out_1.rearrange("g p m t -> g p (m t)").bitcast(I32)
    scales_hbm = out_2.bitcast(I32)

    shot_tiles = [("shots", g, t) for g in range(GROUPS) for t in range(PACK)]
    green_tiles = [("green", n, c) for n in range(STRIPS) for c in range(PASSES)]
    beat_green = [green_tiles[:2], green_tiles[2:4]] + [[item] for item in green_tiles[4 : len(shot_tiles) + 2]]
    late_green = green_tiles[len(shot_tiles) + 2 :]

    units = [(g, n * STRIP, STRIP) for n in range(STRIPS) for g in range(GROUPS)]
    last_g, last_col, last_width = units.pop()
    halves = [(last_g, last_col + first, last_width // 2) for first in (0, last_width // 2)]
    jobs = []
    for unit in units + halves:
        per_bank = BANK // unit[2]
        jobs.extend((unit, tuple(range(t, t + per_bank))) for t in range(0, PACK, per_bank))
    head_jobs = jobs[: GROUPS * PACK]

    with ExitStack() as ctx:
        sbuf = ctx.enter_context(tc.tile_pool(name="sbuf", bufs=1))
        psum = ctx.enter_context(tc.psum_pool(name="psum", bufs=1))
        ctx.enter_context(tc.manual_schedule())

        raw = {}
        woven = {}
        woven_whole = {}
        turned = []
        codes = {}
        factors = {}
        job_banks = {}
        passes_done = {}

        def bank_tile(index):
            return psum.tile([P, BANK], F32, name="bank%d" % index)

        def load(item):
            kind, a, b = item
            if kind == "shots":
                tile = sbuf.tile([P, K], BF16, name="shots_raw", bufs=6)
                nc.sync.dma_start(out=tile[:], in_=shots_hbm[a, b])
            else:
                tile = sbuf.tile([P, PACK, STRIP], BF16, name="green_raw", bufs=8)
                rows = green_kn[b * K_PASS : (b + 1) * K_PASS, a * STRIP : (a + 1) * STRIP]
                nc.sync.dma_start(out=tile[:], in_=rows.rearrange("(p t) w -> p t w", t=PACK))
            raw[item] = tile

        def spread(rows, bank):
            words = rows[:].bitcast(F32)
            count = words.shape[1]
            for m in range(count):
                nc.tensor.transpose(bank[:, m::count], words[:, m : m + 1].to_broadcast([P, P]), identity[:])

        def fetch_gain(side):
            words = slice(side * BANK // 2, (side + 1) * BANK // 2)
            nc.vector.tensor_copy(out=gain_all[:].bitcast(F32)[:, words], in_=gain_bank[:, words])

        def take_woven(things, width, name, bufs):
            tile = sbuf.tile([P, len(things) * PACK * width], BF16, name=name, bufs=bufs, align_bytes=64)
            woven_whole[things[0]] = tile
            for place, thing in enumerate(things):
                woven[thing] = tile[:, place * PACK * width : (place + 1) * PACK * width]

        def take_free(thing, width):
            take_woven([thing], width, "woven", 5)

        def take_gated(things):
            take_woven(things, STRIP, "gated", 1)

        def turn(item):
            words = raw[item][:].bitcast(F32)
            for half in range(2):
                bank = bank_tile(TURN_BANKS[len(turned) % len(TURN_BANKS)])
                for j in range(4):
                    first = 256 * (2 * half + j // 2) + j % 2
                    nc.tensor.transpose(bank[:, j * P : (j + 1) * P], words[:, first : first + 255 : 2], identity[:])
                turned.append(bank)

        def drain(item):
            take_free(item, STRIP)
            words = woven[item].bitcast(F32).rearrange("p (h c m u) -> p h c m u", h=2, c=2, u=2)
            for half, bank in enumerate(turned[-2:]):
                nc.scalar.copy(out=words[:, half], in_=bank[:].rearrange("p (c u m) -> p c m u", c=2, u=2))

        def weave(thing, copy, first, last):
            copy(
                out=woven[thing][:, first * PACK : last * PACK].rearrange("p (c i t) -> p c t i", i=RUN, t=PACK),
                in_=raw[thing][:, :, first:last].rearrange("p t (c i) -> p c t i", i=RUN),
            )

        def pool_weave(thing, last):
            nc.gpsimd.tensor_scalar(
                out=woven[thing][:, : last * PACK].rearrange("p (c t) -> p c t", t=PACK),
                in0=raw[thing][:, :, :last].rearrange("p t c -> p c t"),
                scalar1=1.0,
                scalar2=0.0,
                op0=ALU.mult,
                op1=ALU.add,
            )

        def quantize(items, bufs):
            name = items[0][0] + "%d" % len(items)
            words = sbuf.tile([P, STRIP * len(items)], U32, name=name + "_codes", bufs=bufs, align_bytes=64)
            scales = sbuf.tile([P, STRIP * len(items)], U8, name=name + "_scales", bufs=bufs, align_bytes=64)
            nc.vector.quantize_mx(out=words[:].bitcast(FP8X4), scales=scales[:], in_=woven_whole[items[0]][:])
            for place, item in enumerate(items):
                cols = slice(place * STRIP, (place + 1) * STRIP)
                codes[item] = (words[:, cols], scales[:, cols])

        def multiply(job, place, c):
            (g, col, width), slots = job
            if job not in job_banks:
                index = jobs.index(job)
                late = index - len(head_jobs)
                job_banks[job] = bank_tile(index % PACK if late < 0 else JOB_BANKS[late % len(JOB_BANKS)])
            n, first = divmod(col, STRIP)
            cols = slice(first, first + width)
            green_words, green_scales = codes[("green", n, c)]
            shot_words, shot_scales = codes[("shots", g, slots[place])]
            shots = slice(c * P, (c + 1) * P)
            done = passes_done.setdefault((job, place), [])
            nc.tensor.matmul_mx(
                out=job_banks[job][:, place * width : (place + 1) * width],
                lhsT=shot_words[:, shots].bitcast(FP8X4),
                lhsT_scale=shot_scales[:, shots],
                rhs=green_words[:, cols].bitcast(FP8X4),
                rhs_scale=green_scales[:, cols],
                start=len(done) == 0,
                stop=len(done) == PASSES - 1,
            )
            done.append(c)

        def multiply_all(job):
            for place in range(len(job[1])):
                for c in range(PASSES):
                    multiply(job, place, c)

        def quantize_and_multiply(item):
            quantize([item], len(shot_tiles) if item in shot_tiles else len(green_tiles) - len(late_green))
            for job, shots in zip(head_jobs, shot_tiles):
                for c in range(PASSES):
                    needs = (shots, green_tiles[c])
                    if item in needs and all(need in codes for need in needs):
                        multiply(job, 0, c)

        def exponent(g, side, t):
            if (g, side) not in factors:
                factors[(g, side)] = sbuf.tile([P, PACK, R // 2], F32, name="factor", bufs=3)
            receivers = slice(side * R // 2, (side + 1) * R // 2)
            nc.vector.scalar_tensor_tensor(
                out=factors[(g, side)][:, t, :],
                in0=path_bank[:].bitcast(BF16)[:, receivers],
                scalar=absorb[:, g, t : t + 1],
                in1=gain_all[:, receivers],
                op0=ALU.mult,
                op1=ALU.subtract,
            )

        def exponential(g, side, first, last):
            part = factors[(g, side)][:, first:last, :]
            nc.scalar.activation(out=part, in_=part, func=ACT.Exp, scale=-1.0)

        def scale_out(job):
            unit, slots = job
            g, col, width = unit
            if unit not in raw:
                raw[unit] = sbuf.tile([P, PACK, width], F32, name="y", bufs=5)
            ts = slice(slots[0], slots[-1] + 1)
            side, first = divmod(col, SIDE)
            factor = factors[(g, side)][:, ts, first // 2 : (first + width) // 2]
            nc.vector.tensor_tensor(
                out=raw[unit][:, ts, :].rearrange("p t (r c) -> p t r c", c=2),
                in0=job_banks[job][:].rearrange("p (t r c) -> p t r c", t=len(slots), c=2),
                in1=factor.unsqueeze(3).to_broadcast([P, len(slots), width // 2, 2]),
                op=ALU.mult,
            )
            count = PACK if unit in halves else 2
            if slots[-1] % count == count - 1:
                stored = slice(slots[-1] + 1 - count, slots[-1] + 1)
                nc.sync.dma_start(out=y_hbm[g, :, stored, col : col + width], in_=raw[unit][:, stored, :])

        def quantize_result(parts):
            g, col, width = parts[0]
            width = width * len(parts)
            side, first = divmod(col, SIDE)
            words = sbuf.tile([P, width], U32, name="y_codes", bufs=4, align_bytes=64)
            scales = y_scales[side][4 * g :, first : first + width]
            nc.vector.quantize_mx(out=words[:].bitcast(FP8X4), scales=scales, in_=woven_whole[parts[0]][:])
            nc.sync.dma_start(out=words_hbm[g, :, col : col + width], in_=words[:].bitcast(I32))

        def store_scales(side, queues):
            words = slice(side * SIDE // 4, (side + 1) * SIDE // 4)
            for q in range(4):
                queues[q % len(queues)].dma_start(
                    out=scales_hbm[:, 4 * q : 4 * q + 4, words],
                    in_=y_scales[side][32 * q : 32 * q + 4 * GROUPS].bitcast(I32),
                )

        identity = sbuf.tile([P, P], F32, name="identity")
        make_identity(nc, identity[:])
        gain_rows = sbuf.tile([P, R // P], BF16, name="gain_rows")
        nc.scalar.dma_start(out=gain_rows[:], in_=log_gain.rearrange("(p m) -> p m", p=P))
        path_rows = sbuf.tile([P, R // P], BF16, name="path_rows")
        nc.scalar.dma_start(out=path_rows[:], in_=path.rearrange("(p m) -> p m", p=P))
        absorb = sbuf.tile([P, GROUPS, PACK], BF16, name="absorb")
        nc.scalar.dma_start(out=absorb[:], in_=absorption.rearrange("(g p t) -> p g t", p=P, t=PACK))
        early_scales = sbuf.tile([P, SIDE], U8, name="early_scales", align_bytes=64)
        late_scales = sbuf.tile([P, SIDE], U8, name="late_scales", align_bytes=64)
        y_scales = (early_scales, late_scales)

        beat_loads = [[shots] + items for shots, items in zip(shot_tiles, beat_green)]
        for items in beat_loads[:LOAD_LEAD]:
            for item in items:
                load(item)
        beat_loads = beat_loads[LOAD_LEAD:] + [[]] + [late_green[i : i + 2] for i in range(0, len(late_green), 2)]

        path_bank = bank_tile(PATH_BANK)
        gain_bank = bank_tile(GAIN_BANK)
        gain_all = sbuf.tile([P, R], BF16, name="gain_all")
        spread(gain_rows, gain_bank)
        spread(path_rows, path_bank)
        fetch_gain(0)
        exponent(0, 0, 0)
        exponential(0, 0, 0, 1)
        turn(shot_tiles[0])

        for k, shots in enumerate(shot_tiles):
            for item in beat_loads[k]:
                load(item)
            drain(shots)
            items = beat_green[k]
            if len(items) == 2:
                for item in items:
                    take_free(item, STRIP)
                    weave(item, nc.scalar.copy, VECTOR_COLS_FIRST, STRIP)
                    weave(item, nc.vector.tensor_copy, 0, VECTOR_COLS_FIRST)
                    if item == green_tiles[0]:
                        exponent(0, 0, 1)
                if k == 0:
                    fetch_gain(1)
                turn(shot_tiles[k + 1])
                quantize_and_multiply(shots)
                for item in items:
                    quantize_and_multiply(item)
                if k == 0:
                    exponential(0, 0, 1, 2)
                continue
            if len(beat_green[k - 1]) == 1:
                quantize_and_multiply(beat_green[k - 1][0])
            take_gated(items)
            with_product = 0 <= k - SCALE_LAG < PACK
            if with_product:
                pool_weave(items[0], POOL_COLS_HEAD)
            weave(items[0], nc.scalar.copy, POOL_COLS_HEAD + VECTOR_COLS_HEAD, STRIP)
            if with_product:
                scale_out(jobs[k - SCALE_LAG])
            g, t = divmod(k, PACK)
            exponent(g, 0, t)
            weave(items[0], nc.vector.tensor_copy, POOL_COLS_HEAD if with_product else 0, POOL_COLS_HEAD + VECTOR_COLS_HEAD)
            if k + 1 < len(shot_tiles):
                turn(shot_tiles[k + 1])
            else:
                multiply_all(jobs[len(head_jobs)])
            quantize_and_multiply(shots)
            exponential(g, 0, t, t + 1)
        quantize_and_multiply(beat_green[-1][0])

        pairs = [late_green[i : i + 2] for i in range(0, len(late_green), 2)] + [[units[0], units[GROUPS]]]
        for u in range(1, len(units)):
            for job in jobs[PACK * u : PACK * (u + 1)]:
                scale_out(job)
            for job in jobs[PACK * (u + 1) : PACK * (u + 2)]:
                if job not in job_banks:
                    multiply_all(job)
            if u <= len(pairs):
                g, t = divmod(2 * (u - 1), PACK)
                exponent(g, 1, t)
                exponent(g, 1, t + 1)
            strip, half = divmod(u - 2, 2)
            halved = units[GROUPS * strip + 1] if 0 <= strip < 2 else None
            if halved:
                if half == 0:
                    take_free(halved, STRIP)
                weave(halved, nc.scalar.copy, half * STRIP // 2, (half + 1) * STRIP // 2)
            if u <= len(pairs):
                gated = pairs[u - 1]
                take_gated(gated)
                pool_weave(gated[0], STRIP)
                weave(gated[1], nc.scalar.copy, 0, STRIP)
                exponential(g, 1, t, t + 2)
            else:
                gated = [units[u - 1]]
                take_gated(gated)
                pool_weave(gated[0], POOL_COLS_SHORT)
                weave(gated[0], nc.scalar.copy, POOL_COLS_SHORT, STRIP)
            if halved and half == 1:
                quantize_result([halved])
                if strip == 1:
                    store_scales(0, [nc.sync])
            if gated[0] in late_green:
                quantize(gated, len(late_green) // 2)
            else:
                quantize_result(gated)

        first_half, second_half = halves
        width = first_half[2]
        for job in jobs[-4:-2]:
            scale_out(job)
        take_gated([units[-1]])
        pool_weave(units[-1], POOL_COLS_SHORT)
        weave(units[-1], nc.scalar.copy, POOL_COLS_SHORT, STRIP)
        take_free(first_half, width)
        weave(first_half, nc.scalar.copy, 0, width)
        for job in jobs[-2:]:
            scale_out(job)
        quantize_result([units[-1]])
        quantize_result([first_half])
        take_free(second_half, width)
        weave(second_half, nc.scalar.copy, VECTOR_COLS_LAST, width)
        weave(second_half, nc.vector.tensor_copy, 0, VECTOR_COLS_LAST)
        quantize_result([second_half])
        store_scales(1, [nc.scalar, nc.sync])
